import numpy as np
import ml_dtypes


def mxq(x, axis, fmt="e4m3"):
    dtype, down = {"e4m3": (ml_dtypes.float8_e4m3fn, 7), "e5m2": (ml_dtypes.float8_e5m2, 14)}[fmt]
    v = np.moveaxis(np.asarray(x, np.float32).astype(ml_dtypes.bfloat16).astype(np.float64), axis, -1)
    blocks = v.reshape(v.shape[:-1] + (-1, 32))
    amax = np.abs(blocks).max(-1, keepdims=True)
    byte = np.maximum(np.where(amax > 0, np.frexp(amax)[1] - 1 + 127, 0) - down, 1)
    scale = np.exp2(byte - 127.0)
    codes = (blocks / scale).astype(np.float32).astype(dtype).astype(np.float64)
    return np.moveaxis((codes * scale).reshape(v.shape), -1, axis)


WIDE = False


def mx_kscale(k):
    if not WIDE:
        return np.ones(k)
    levels = np.array([10, -10, 5, -5, 0])
    if k % 512:
        return np.exp2(np.random.permutation(np.resize(levels, k // 32))).repeat(32)
    a = np.empty((k // 512, 16))
    for p in range(k // 512):
        a[p, :8] = np.random.permutation(np.resize(levels, 8))
        for g in range(8):
            far = levels[np.abs(levels - a[p, g]) >= 10]
            a[p, g + 8] = far[np.random.randint(len(far))]
    return np.exp2(a.ravel()).repeat(32)


def f64(x):
    return np.asarray(x).astype(np.float64)


def striped(idx):
    return np.tile(idx.reshape(-1, 16).T, (8, 1)).astype(np.uint16)


def unstriped(offs):
    return offs[:16].T.reshape(-1).astype(np.int64)


def relu(v):
    return np.maximum(v, 0.0)


K, T, S, V, N = 1024, 2048, 512, 256, 128


def setup_inputs():
    n = np.random.standard_normal
    s = mx_kscale(K)[:, None]
    return {
        "xT": (n((K, T)) * s).astype(np.float32),
        "w1": (n((K, N)) / np.sqrt(K) / s).astype(np.float32),
        "w2": (n((K, N)) / np.sqrt(K) / s).astype(np.float32),
        "w3": (n((K, N)) / np.sqrt(K) / s).astype(np.float32),
        "offs": striped(np.random.permutation(T)[:S]),
        "cen": striped(np.random.permutation(S)[:V]),
        "pos1": striped(np.random.permutation(S)[:V]),
        "pos2": striped(np.random.permutation(S)[:V]),
    }


def reference(xT, w1, w2, w3, offs, cen, pos1, pos2):
    xq = mxq(f64(xT)[:, unstriped(offs)], 0, "e4m3")
    h = mxq(f64(w3), 0, "e4m3").T @ xq
    g = mxq(f64(w1), 0, "e4m3").T @ xq
    gc = g[:, unstriped(cen)]
    s = mxq(f64(w2), 0, "e4m3").T @ xq
    sc = s[:, unstriped(cen)]
    return relu(h[:, unstriped(pos1)] * gc + sc) + relu(h[:, unstriped(pos2)] * gc + sc)

@@ -1,0 +1,166 @@
+from contextlib import ExitStack
+
+import concourse.mybir as mybir
+
+K, T, S, V, N = 1024, 2048, 512, 256, 128
+FLOPS = 3 * 2 * K * S * N
+
+F32 = mybir.dt.float32
+BF16 = mybir.dt.bfloat16
+U32 = mybir.dt.uint32
+U16 = mybir.dt.uint16
+U8 = mybir.dt.uint8
+FP8X4 = mybir.dt.float8_e4m3fn_x4
+ALU = mybir.AluOpType
+ACT = mybir.ActivationFunctionType
+
+P = 128
+PACK = 4
+K_PASS = P * PACK
+PASSES = K // K_PASS
+HALF = S // 2
+QUARTER = S // 4
+COLS16 = 16
+
+
+def tile_picked_filmg_relu_e_kernel(tc, xT, w1, w2, w3, offs, cen, pos1, pos2, out):
+    nc = tc.nc
+    with ExitStack() as ctx:
+        keep = ctx.enter_context(tc.tile_pool(name="keep", bufs=1))
+        psum = ctx.enter_context(tc.psum_pool(name="psum", bufs=1))
+
+        offs_t = keep.tile([P, S // COLS16], U16, name="offs_t")
+        cen_t = keep.tile([P, V // COLS16], U16, name="cen_t")
+        pos1_t = keep.tile([P, V // COLS16], U16, name="pos1_t")
+        pos2_t = keep.tile([P, V // COLS16], U16, name="pos2_t")
+
+        x_rows = xT.rearrange("(z p j) t -> z j p t", z=PASSES, j=PACK)
+        plane = [[keep.tile([P, T], F32, name=f"plane{z}{j}") for j in range(PACK)] for z in range(PASSES)]
+        weights = {"g": w1, "s": w2, "h": w3}
+        w_raw = {(m, z): keep.tile([P, PACK, N], F32, name=f"wraw_{m}{z}") for m in weights for z in range(PASSES)}
+        w_il = {(m, z): keep.tile([P, N, PACK], BF16, name=f"wil_{m}{z}", align_bytes=64) for m in weights for z in range(PASSES)}
+        w_codes = {(m, z): keep.tile([P, N], U32, name=f"wc_{m}{z}", align_bytes=64) for m in weights for z in range(PASSES)}
+        w_scales = {(m, z): keep.tile([P, N], U8, name=f"ws_{m}{z}", align_bytes=64) for m in weights for z in range(PASSES)}
+
+        def load_plane(z, j):
+            nc.sync.dma_start(out=plane[z][j][:], in_=x_rows[z, j])
+
+        def load_w(m, z):
+            rows = weights[m][z * K_PASS:(z + 1) * K_PASS, :]
+            nc.sync.dma_start(out=w_raw[m, z][:], in_=rows.rearrange("(p j) c -> p j c", j=PACK))
+
+        load_plane(0, 0)
+        nc.sync.dma_start(offs_t[:], offs)
+        load_plane(0, 1)
+        load_w("g", 0)
+        load_w("g", 1)
+        load_plane(0, 2)
+        load_plane(0, 3)
+        for j in range(PACK):
+            load_plane(1, j)
+        load_w("s", 0)
+        load_w("s", 1)
+        nc.sync.dma_start(cen_t[:], cen)
+        load_w("h", 0)
+        load_w("h", 1)
+        nc.sync.dma_start(pos1_t[:], pos1)
+        nc.sync.dma_start(pos2_t[:], pos2)
+
+        def round_w(m, z):
+            nc.scalar.copy(
+                out=w_il[m, z][:].rearrange("p (c i) j -> p c j i", i=4),
+                in_=w_raw[m, z][:].rearrange("p j (c i) -> p c j i", i=4),
+            )
+
+        def quant_w(m, z):
+            nc.vector.quantize_mx(
+                out=w_codes[m, z][:].bitcast(FP8X4),
+                scales=w_scales[m, z][:],
+                in_=w_il[m, z][:].rearrange("p c j -> p (c j)"),
+            )
+
+        x_codes = [keep.tile([P, S], U32, name=f"xc{z}", align_bytes=64) for z in range(PASSES)]
+        x_scales = [keep.tile([P, S], U8, name=f"xs{z}", align_bytes=64) for z in range(PASSES)]
+        x_il0 = keep.tile([P, S, PACK], BF16, name="xil0", align_bytes=64)
+        x_il1 = [keep.tile([P, HALF, PACK], BF16, name=f"xil1_{a}", align_bytes=64) for a in range(2)]
+
+        def quant_x(z, src, c0, c1):
+            nc.vector.quantize_mx(
+                out=x_codes[z][:, c0:c1].bitcast(FP8X4),
+                scales=x_scales[z][:, c0:c1],
+                in_=src.rearrange("p c j -> p (c j)"),
+            )
+
+        def mm(bank, m, z, c0, c1):
+            nc.tensor.matmul_mx(
+                out=bank,
+                lhsT=w_codes[m, z][:].bitcast(FP8X4),
+                lhsT_scale=w_scales[m, z][:],
+                rhs=x_codes[z][:, c0:c1].bitcast(FP8X4),
+                rhs_scale=x_scales[z][:, c0:c1],
+                start=(z == 0),
+                stop=(z == PASSES - 1),
+            )
+
+        for z in range(PASSES):
+            round_w("g", z)
+            quant_w("g", z)
+
+        for j in range(PACK):
+            nc.vector.tensor_copy(out=x_il0[:, :, j], in_=plane[0][j][:].indirect(offs_t[:]))
+        quant_x(0, x_il0[:], 0, S)
+
+        g_cuts = [(0, HALF), (HALF, HALF + QUARTER), (HALF + QUARTER, S)]
+        g_bank = [psum.tile([P, c1 - c0], F32, name=f"g_bank{i}") for i, (c0, c1) in enumerate(g_cuts)]
+        s_bank = psum.tile([P, S], F32, name="s_bank")
+        h_bank = psum.tile([P, S], F32, name="h_bank")
+        for i, (c0, c1) in enumerate(g_cuts):
+            mm(g_bank[i][:], "g", 0, c0, c1)
+
+        for j in range(PACK):
+            for a in range(2):
+                lst = offs_t[:, a * HALF // COLS16:(a + 1) * HALF // COLS16]
+                nc.vector.tensor_copy(out=x_il1[a][:, :, j], in_=plane[1][j][:].indirect(lst))
+        quant_x(1, x_il1[0][:], 0, HALF)
+        quant_x(1, x_il1[1][:, 0:QUARTER, :], HALF, HALF + QUARTER)
+        quant_x(1, x_il1[1][:, QUARTER:HALF, :], HALF + QUARTER, S)
+
+        g_sb = keep.tile([P, S], F32, name="g_sb")
+        s_sb = keep.tile([P, S], F32, name="s_sb")
+        h_sb = keep.tile([P, S], F32, name="h_sb")
+
+        for z in range(PASSES):
+            round_w("s", z)
+        round_w("h", 0)
+        for i, (c0, c1) in enumerate(g_cuts):
+            mm(g_bank[i][:], "g", 1, c0, c1)
+            nc.scalar.copy(out=g_sb[:, c0:c1], in_=g_bank[i][:])
+        round_w("h", 1)
+        for z in range(PASSES):
+            quant_w("s", z)
+            mm(s_bank[:], "s", z, 0, S)
+        quant_w("h", 0)
+        mm(h_bank[:], "h", 0, 0, S)
+
+        gc = keep.tile([P, V], F32, name="gc")
+        sc = keep.tile([P, V], F32, name="sc")
+        t1 = keep.tile([P, V], F32, name="t1")
+        t2 = keep.tile([P, V], F32, name="t2")
+        u1 = keep.tile([P, V], F32, name="u1")
+        u2 = keep.tile([P, V], F32, name="u2")
+        r1 = keep.tile([P, V], F32, name="r1")
+        res = keep.tile([P, V], F32, name="res")
+
+        nc.vector.tensor_copy(out=gc[:], in_=g_sb[:].indirect(cen_t[:]))
+        nc.scalar.copy(out=s_sb[:], in_=s_bank[:])
+        quant_w("h", 1)
+        mm(h_bank[:], "h", 1, 0, S)
+        nc.scalar.copy(out=h_sb[:], in_=h_bank[:])
+        nc.vector.tensor_copy(out=sc[:], in_=s_sb[:].indirect(cen_t[:]))
+        nc.vector.tensor_tensor(t1[:], h_sb[:].indirect(pos1_t[:]), gc[:], ALU.mult)
+        nc.vector.tensor_tensor(t2[:], h_sb[:].indirect(pos2_t[:]), gc[:], ALU.mult)
+        nc.vector.tensor_tensor(u1[:], t1[:], sc[:], ALU.add)
+        nc.vector.tensor_tensor(u2[:], t2[:], sc[:], ALU.add)
+        nc.scalar.activation(out=r1[:], in_=u1[:], func=ACT.Relu)
+        nc.vector.scalar_tensor_tensor(out=res[:], in0=u2[:], scalar=0.0, in1=r1[:], op0=ALU.max, op1=ALU.add)
+        nc.sync.dma_start(out=out, in_=res[:])

@@ -34,35 +34,37 @@ def tile_picked_filmg_relu_e_kernel(tc, xT, w1, w2, w3, offs, cen, pos1, pos2, o
         pos1_t = keep.tile([P, V // COLS16], U16, name="pos1_t")
         pos2_t = keep.tile([P, V // COLS16], U16, name="pos2_t")
 
-        x_rows = xT.rearrange("(z p j) t -> z j p t", z=PASSES, j=PACK)
-        plane = [[keep.tile([P, T], F32, name=f"plane{z}{j}") for j in range(PACK)] for z in range(PASSES)]
+        x_rows = xT.rearrange("(z p j) t -> z p j t", z=PASSES, j=PACK)
+        loads = [(0, 0, 2), (0, 2, 2), (1, 0, 2), (1, 2, 1), (1, 3, 1)]
+        x_tiles = [keep.tile([P, n, T], F32, name=f"x{z}{j}") for z, j, n in loads]
+        plane = {(z, j + i): x_tiles[q][:, i, :] for q, (z, j, n) in enumerate(loads) for i in range(n)}
         weights = {"g": w1, "s": w2, "h": w3}
-        w_raw = {(m, z): keep.tile([P, PACK, N], F32, name=f"wraw_{m}{z}") for m in weights for z in range(PASSES)}
-        w_il = {(m, z): keep.tile([P, N, PACK], BF16, name=f"wil_{m}{z}", align_bytes=64) for m in weights for z in range(PASSES)}
+        w_raw = {(m, z): keep.tile([P, PACK, N], F32, name=f"wraw_{m}{z}", tag=f"wraw_{m}{z}") for m in weights for z in range(PASSES)}
+        w_il = {(m, z): keep.tile([P, N, PACK], BF16, name=f"wil_{m}{z}", tag=f"wil_{m}{z}", align_bytes=64) for m in weights for z in range(PASSES)}
         w_codes = {(m, z): keep.tile([P, N], U32, name=f"wc_{m}{z}", align_bytes=64) for m in weights for z in range(PASSES)}
         w_scales = {(m, z): keep.tile([P, N], U8, name=f"ws_{m}{z}", align_bytes=64) for m in weights for z in range(PASSES)}
 
-        def load_plane(z, j):
-            nc.sync.dma_start(out=plane[z][j][:], in_=x_rows[z, j])
+        def load_x(q):
+            z, j, n = loads[q]
+            nc.sync.dma_start(out=x_tiles[q][:], in_=x_rows[z, :, j:j + n, :])
 
         def load_w(m, z):
             rows = weights[m][z * K_PASS:(z + 1) * K_PASS, :]
             nc.sync.dma_start(out=w_raw[m, z][:], in_=rows.rearrange("(p j) c -> p j c", j=PACK))
 
-        load_plane(0, 0)
+        load_x(0)
         nc.sync.dma_start(offs_t[:], offs)
-        load_plane(0, 1)
+        load_x(1)
+        load_x(2)
         load_w("g", 0)
         load_w("g", 1)
-        load_plane(0, 2)
-        load_plane(0, 3)
-        for j in range(PACK):
-            load_plane(1, j)
         load_w("s", 0)
-        load_w("s", 1)
-        nc.sync.dma_start(cen_t[:], cen)
         load_w("h", 0)
+        load_x(3)
+        load_x(4)
+        load_w("s", 1)
         load_w("h", 1)
+        nc.sync.dma_start(cen_t[:], cen)
         nc.sync.dma_start(pos1_t[:], pos1)
         nc.sync.dma_start(pos2_t[:], pos2)
 
@@ -102,45 +104,47 @@ def tile_picked_filmg_relu_e_kernel(tc, xT, w1, w2, w3, offs, cen, pos1, pos2, o
                 stop=(z == PASSES - 1),
             )
 
-        for z in range(PASSES):
-            round_w("g", z)
-            quant_w("g", z)
-
         for j in range(PACK):
-            nc.vector.tensor_copy(out=x_il0[:, :, j], in_=plane[0][j][:].indirect(offs_t[:]))
+            nc.vector.tensor_copy(out=x_il0[:, :, j], in_=plane[0, j].indirect(offs_t[:]))
         quant_x(0, x_il0[:], 0, S)
 
-        g_cuts = [(0, HALF), (HALF, HALF + QUARTER), (HALF + QUARTER, S)]
-        g_bank = [psum.tile([P, c1 - c0], F32, name=f"g_bank{i}") for i, (c0, c1) in enumerate(g_cuts)]
-        s_bank = psum.tile([P, S], F32, name="s_bank")
-        h_bank = psum.tile([P, S], F32, name="h_bank")
-        for i, (c0, c1) in enumerate(g_cuts):
-            mm(g_bank[i][:], "g", 0, c0, c1)
+        cuts = {
+            "g": [(c, c + QUARTER) for c in range(0, S, QUARTER)],
+            "s": [(0, HALF), (HALF, S)],
+            "h": [(0, HALF), (HALF, S)],
+        }
+        bank = {(m, c0): psum.tile([P, c1 - c0], F32, name=f"bank_{m}{c0}") for m in cuts for c0, c1 in cuts[m]}
 
-        for j in range(PACK):
+        def gather_pass1(j):
             for a in range(2):
                 lst = offs_t[:, a * HALF // COLS16:(a + 1) * HALF // COLS16]
-                nc.vector.tensor_copy(out=x_il1[a][:, :, j], in_=plane[1][j][:].indirect(lst))
-        quant_x(1, x_il1[0][:], 0, HALF)
-        quant_x(1, x_il1[1][:, 0:QUARTER, :], HALF, HALF + QUARTER)
-        quant_x(1, x_il1[1][:, QUARTER:HALF, :], HALF + QUARTER, S)
+                nc.vector.tensor_copy(out=x_il1[a][:, :, j], in_=plane[1, j].indirect(lst))
 
-        g_sb = keep.tile([P, S], F32, name="g_sb")
-        s_sb = keep.tile([P, S], F32, name="s_sb")
-        h_sb = keep.tile([P, S], F32, name="h_sb")
+        gather_pass1(0)
+        gather_pass1(1)
+        for m, z in (("g", 0), ("g", 1), ("s", 0), ("h", 0)):
+            round_w(m, z)
+            quant_w(m, z)
+        for m in cuts:
+            for c0, c1 in cuts[m]:
+                mm(bank[m, c0][:], m, 0, c0, c1)
+        gather_pass1(2)
+        gather_pass1(3)
+        for c0, c1 in cuts["g"]:
+            quant_x(1, x_il1[c0 // HALF][:, c0 % HALF:c0 % HALF + QUARTER, :], c0, c1)
+        for m in ("s", "h"):
+            round_w(m, 1)
+            quant_w(m, 1)
 
-        for z in range(PASSES):
-            round_w("s", z)
-        round_w("h", 0)
-        for i, (c0, c1) in enumerate(g_cuts):
-            mm(g_bank[i][:], "g", 1, c0, c1)
-            nc.scalar.copy(out=g_sb[:, c0:c1], in_=g_bank[i][:])
-        round_w("h", 1)
-        for z in range(PASSES):
-            quant_w("s", z)
-            mm(s_bank[:], "s", z, 0, S)
-        quant_w("h", 0)
-        mm(h_bank[:], "h", 0, 0, S)
+        prod = {
+            "g": keep.tile([P, S], F32, name="g_sb", tag="wraw_h1"),
+            "s": keep.tile([P, S], F32, name="s_sb", tag="wil_h1", align_bytes=64),
+            "h": keep.tile([P, S], F32, name="h_sb"),
+        }
+        for m in cuts:
+            for c0, c1 in cuts[m]:
+                mm(bank[m, c0][:], m, 1, c0, c1)
+                nc.scalar.copy(out=prod[m][:, c0:c1], in_=bank[m, c0][:])
 
         gc = keep.tile([P, V], F32, name="gc")
         sc = keep.tile([P, V], F32, name="sc")
@@ -151,14 +155,10 @@ def tile_picked_filmg_relu_e_kernel(tc, xT, w1, w2, w3, offs, cen, pos1, pos2, o
         r1 = keep.tile([P, V], F32, name="r1")
         res = keep.tile([P, V], F32, name="res")
 
-        nc.vector.tensor_copy(out=gc[:], in_=g_sb[:].indirect(cen_t[:]))
-        nc.scalar.copy(out=s_sb[:], in_=s_bank[:])
-        quant_w("h", 1)
-        mm(h_bank[:], "h", 1, 0, S)
-        nc.scalar.copy(out=h_sb[:], in_=h_bank[:])
-        nc.vector.tensor_copy(out=sc[:], in_=s_sb[:].indirect(cen_t[:]))
-        nc.vector.tensor_tensor(t1[:], h_sb[:].indirect(pos1_t[:]), gc[:], ALU.mult)
-        nc.vector.tensor_tensor(t2[:], h_sb[:].indirect(pos2_t[:]), gc[:], ALU.mult)
+        nc.vector.tensor_copy(out=gc[:], in_=prod["g"][:].indirect(cen_t[:]))
+        nc.vector.tensor_copy(out=sc[:], in_=prod["s"][:].indirect(cen_t[:]))
+        nc.vector.tensor_tensor(t1[:], prod["h"][:].indirect(pos1_t[:]), gc[:], ALU.mult)
+        nc.vector.tensor_tensor(t2[:], prod["h"][:].indirect(pos2_t[:]), gc[:], ALU.mult)
         nc.vector.tensor_tensor(u1[:], t1[:], sc[:], ALU.add)
         nc.vector.tensor_tensor(u2[:], t2[:], sc[:], ALU.add)
         nc.scalar.activation(out=r1[:], in_=u1[:], func=ACT.Relu)

@@ -39,7 +39,7 @@ def tile_picked_filmg_relu_e_kernel(tc, xT, w1, w2, w3, offs, cen, pos1, pos2, o
         x_tiles = [keep.tile([P, n, T], F32, name=f"x{z}{j}") for z, j, n in loads]
         plane = {(z, j + i): x_tiles[q][:, i, :] for q, (z, j, n) in enumerate(loads) for i in range(n)}
         weights = {"g": w1, "s": w2, "h": w3}
-        w_raw = {(m, z): keep.tile([P, PACK, N], F32, name=f"wraw_{m}{z}", tag=f"wraw_{m}{z}") for m in weights for z in range(PASSES)}
+        w_raw = {(m, z): keep.tile([P, PACK, N], F32, name=f"wraw_{m}{z}", tag=f"wraw_{m}{z}", align_bytes=64) for m in weights for z in range(PASSES)}
         w_il = {(m, z): keep.tile([P, N, PACK], BF16, name=f"wil_{m}{z}", tag=f"wil_{m}{z}", align_bytes=64) for m in weights for z in range(PASSES)}
         w_codes = {(m, z): keep.tile([P, N], U32, name=f"wc_{m}{z}", align_bytes=64) for m in weights for z in range(PASSES)}
         w_scales = {(m, z): keep.tile([P, N], U8, name=f"ws_{m}{z}", align_bytes=64) for m in weights for z in range(PASSES)}
@@ -57,11 +57,11 @@ def tile_picked_filmg_relu_e_kernel(tc, xT, w1, w2, w3, offs, cen, pos1, pos2, o
         load_x(1)
         load_x(2)
         load_w("g", 0)
-        load_w("g", 1)
         load_w("s", 0)
         load_w("h", 0)
         load_x(3)
         load_x(4)
+        load_w("g", 1)
         load_w("s", 1)
         load_w("h", 1)
         nc.sync.dma_start(cen_t[:], cen)
@@ -81,7 +81,7 @@ def tile_picked_filmg_relu_e_kernel(tc, xT, w1, w2, w3, offs, cen, pos1, pos2, o
                 in_=w_il[m, z][:].rearrange("p c j -> p (c j)"),
             )
 
-        x_codes = [keep.tile([P, S], U32, name=f"xc{z}", align_bytes=64) for z in range(PASSES)]
+        x_codes = [keep.tile([P, S], U32, name="xc0", align_bytes=64)]
         x_scales = [keep.tile([P, S], U8, name=f"xs{z}", align_bytes=64) for z in range(PASSES)]
         x_il0 = keep.tile([P, S, PACK], BF16, name="xil0", align_bytes=64)
         x_il1 = [keep.tile([P, HALF, PACK], BF16, name=f"xil1_{a}", align_bytes=64) for a in range(2)]
@@ -122,7 +122,7 @@ def tile_picked_filmg_relu_e_kernel(tc, xT, w1, w2, w3, offs, cen, pos1, pos2, o
 
         gather_pass1(0)
         gather_pass1(1)
-        for m, z in (("g", 0), ("g", 1), ("s", 0), ("h", 0)):
+        for m, z in (("g", 0), ("s", 0), ("h", 0)):
             round_w(m, z)
             quant_w(m, z)
         for m in cuts:
@@ -130,6 +130,9 @@ def tile_picked_filmg_relu_e_kernel(tc, xT, w1, w2, w3, offs, cen, pos1, pos2, o
                 mm(bank[m, c0][:], m, 0, c0, c1)
         gather_pass1(2)
         gather_pass1(3)
+        round_w("g", 1)
+        quant_w("g", 1)
+        x_codes.append(keep.tile([P, S], U32, name="xc1", tag="wraw_g1", align_bytes=64))
         for c0, c1 in cuts["g"]:
             quant_x(1, x_il1[c0 // HALF][:, c0 % HALF:c0 % HALF + QUARTER, :], c0, c1)
         for m in ("s", "h"):
@@ -137,7 +140,7 @@ def tile_picked_filmg_relu_e_kernel(tc, xT, w1, w2, w3, offs, cen, pos1, pos2, o
             quant_w(m, 1)
 
         prod = {
-            "g": keep.tile([P, S], F32, name="g_sb", tag="wraw_h1"),
+            "g": keep.tile([P, S], F32, name="g_sb", tag="wraw_h1", align_bytes=64),
             "s": keep.tile([P, S], F32, name="s_sb", tag="wil_h1", align_bytes=64),
             "h": keep.tile([P, S], F32, name="h_sb"),
         }
@@ -152,8 +155,8 @@ def tile_picked_filmg_relu_e_kernel(tc, xT, w1, w2, w3, offs, cen, pos1, pos2, o
         t2 = keep.tile([P, V], F32, name="t2")
         u1 = keep.tile([P, V], F32, name="u1")
         u2 = keep.tile([P, V], F32, name="u2")
-        r1 = keep.tile([P, V], F32, name="r1")
-        res = keep.tile([P, V], F32, name="res")
+        r1 = [keep.tile([P, V // 2], F32, name=f"r1_{a}") for a in range(2)]
+        res = [keep.tile([P, V // 2], F32, name=f"res_{a}") for a in range(2)]
 
         nc.vector.tensor_copy(out=gc[:], in_=prod["g"][:].indirect(cen_t[:]))
         nc.vector.tensor_copy(out=sc[:], in_=prod["s"][:].indirect(cen_t[:]))
@@ -161,6 +164,9 @@ def tile_picked_filmg_relu_e_kernel(tc, xT, w1, w2, w3, offs, cen, pos1, pos2, o
         nc.vector.tensor_tensor(t2[:], prod["h"][:].indirect(pos2_t[:]), gc[:], ALU.mult)
         nc.vector.tensor_tensor(u1[:], t1[:], sc[:], ALU.add)
         nc.vector.tensor_tensor(u2[:], t2[:], sc[:], ALU.add)
-        nc.scalar.activation(out=r1[:], in_=u1[:], func=ACT.Relu)
-        nc.vector.scalar_tensor_tensor(out=res[:], in0=u2[:], scalar=0.0, in1=r1[:], op0=ALU.max, op1=ALU.add)
-        nc.sync.dma_start(out=out, in_=res[:])
+        halves = [slice(0, V // 2), slice(V // 2, V)]
+        for a in range(2):
+            nc.scalar.activation(out=r1[a][:], in_=u1[:, halves[a]], func=ACT.Relu)
+        for a in range(2):
+            nc.vector.scalar_tensor_tensor(out=res[a][:], in0=u2[:, halves[a]], scalar=0.0, in1=r1[a][:], op0=ALU.max, op1=ALU.add)
+            nc.sync.dma_start(out=out[:, halves[a]], in_=res[a][:])

@@ -18,7 +18,6 @@ P = 128
 PACK = 4
 K_PASS = P * PACK
 PASSES = K // K_PASS
-HALF = S // 2
 QUARTER = S // 4
 COLS16 = 16
 
@@ -35,14 +34,14 @@ def tile_picked_filmg_relu_e_kernel(tc, xT, w1, w2, w3, offs, cen, pos1, pos2, o
         pos2_t = keep.tile([P, V // COLS16], U16, name="pos2_t")
 
         x_rows = xT.rearrange("(z p j) t -> z p j t", z=PASSES, j=PACK)
-        loads = [(0, 0, 2), (0, 2, 2), (1, 0, 2), (1, 2, 1), (1, 3, 1)]
+        loads = [(0, 0, 2), (0, 2, 2), (1, 0, 1), (1, 1, 1), (1, 2, 1), (1, 3, 1)]
         x_tiles = [keep.tile([P, n, T], F32, name=f"x{z}{j}") for z, j, n in loads]
         plane = {(z, j + i): x_tiles[q][:, i, :] for q, (z, j, n) in enumerate(loads) for i in range(n)}
         weights = {"g": w1, "s": w2, "h": w3}
         w_raw = {(m, z): keep.tile([P, PACK, N], F32, name=f"wraw_{m}{z}", tag=f"wraw_{m}{z}", align_bytes=64) for m in weights for z in range(PASSES)}
-        w_il = {(m, z): keep.tile([P, N, PACK], BF16, name=f"wil_{m}{z}", tag=f"wil_{m}{z}", align_bytes=64) for m in weights for z in range(PASSES)}
-        w_codes = {(m, z): keep.tile([P, N], U32, name=f"wc_{m}{z}", align_bytes=64) for m in weights for z in range(PASSES)}
-        w_scales = {(m, z): keep.tile([P, N], U8, name=f"ws_{m}{z}", align_bytes=64) for m in weights for z in range(PASSES)}
+        w_il = {}
+        w_codes = {}
+        w_scales = {(m, z): keep.tile([P, N], U8, name=f"ws_{m}{z}", tag=f"ws_{m}{z}", align_bytes=64) for m in weights for z in range(PASSES)}
 
         def load_x(q):
             z, j, n = loads[q]
@@ -54,27 +53,25 @@ def tile_picked_filmg_relu_e_kernel(tc, xT, w1, w2, w3, offs, cen, pos1, pos2, o
 
         load_x(0)
         nc.sync.dma_start(offs_t[:], offs)
-        load_x(1)
-        load_x(2)
+        for q in range(1, 5):
+            load_x(q)
         load_w("g", 0)
-        load_w("s", 0)
-        load_w("h", 0)
-        load_x(3)
-        load_x(4)
-        load_w("g", 1)
-        load_w("s", 1)
-        load_w("h", 1)
+        load_x(5)
+        for m, z in (("g", 1), ("h", 0), ("h", 1), ("s", 0), ("s", 1)):
+            load_w(m, z)
         nc.sync.dma_start(cen_t[:], cen)
         nc.sync.dma_start(pos1_t[:], pos1)
         nc.sync.dma_start(pos2_t[:], pos2)
 
-        def round_w(m, z):
-            nc.scalar.copy(
+        def round_w(m, z, copy, tag):
+            w_il[m, z] = keep.tile([P, N, PACK], BF16, name=f"wil_{m}{z}", tag=tag, align_bytes=64)
+            copy(
                 out=w_il[m, z][:].rearrange("p (c i) j -> p c j i", i=4),
                 in_=w_raw[m, z][:].rearrange("p j (c i) -> p c j i", i=4),
             )
 
-        def quant_w(m, z):
+        def quant_w(m, z, tag):
+            w_codes[m, z] = keep.tile([P, N], U32, name=f"wc_{m}{z}", tag=tag, align_bytes=64)
             nc.vector.quantize_mx(
                 out=w_codes[m, z][:].bitcast(FP8X4),
                 scales=w_scales[m, z][:],
@@ -83,8 +80,7 @@ def tile_picked_filmg_relu_e_kernel(tc, xT, w1, w2, w3, offs, cen, pos1, pos2, o
 
         x_codes = [keep.tile([P, S], U32, name="xc0", align_bytes=64)]
         x_scales = [keep.tile([P, S], U8, name=f"xs{z}", align_bytes=64) for z in range(PASSES)]
-        x_il0 = keep.tile([P, S, PACK], BF16, name="xil0", align_bytes=64)
-        x_il1 = [keep.tile([P, HALF, PACK], BF16, name=f"xil1_{a}", align_bytes=64) for a in range(2)]
+        x_il = [keep.tile([P, S, PACK], BF16, name=f"xil{z}", align_bytes=64) for z in range(PASSES)]
 
         def quant_x(z, src, c0, c1):
             nc.vector.quantize_mx(
@@ -104,69 +100,66 @@ def tile_picked_filmg_relu_e_kernel(tc, xT, w1, w2, w3, offs, cen, pos1, pos2, o
                 stop=(z == PASSES - 1),
             )
 
+        def gather_x(z, j):
+            nc.vector.tensor_copy(out=x_il[z][:, :, j], in_=plane[z, j].indirect(offs_t[:]))
+
+        cuts = [(c, c + QUARTER) for c in range(0, S, QUARTER)]
+        prod = {m: keep.tile([P, S], F32, name=f"{m}_sb") for m in weights}
+
+        def banks(m, tag):
+            return {c0: psum.tile([P, QUARTER], F32, name=f"bank_{m}{c0}", tag=f"{tag}{c0}") for c0, c1 in cuts}
+
+        def product(m, bank, passes, copy):
+            for c0, c1 in cuts:
+                for z in passes:
+                    mm(bank[c0][:], m, z, c0, c1)
+                if PASSES - 1 in passes:
+                    copy(out=prod[m][:, c0:c1], in_=bank[c0][:])
+
         for j in range(PACK):
-            nc.vector.tensor_copy(out=x_il0[:, :, j], in_=plane[0, j].indirect(offs_t[:]))
-        quant_x(0, x_il0[:], 0, S)
-
-        cuts = {
-            "g": [(c, c + QUARTER) for c in range(0, S, QUARTER)],
-            "s": [(0, HALF), (HALF, S)],
-            "h": [(0, HALF), (HALF, S)],
-        }
-        bank = {(m, c0): psum.tile([P, c1 - c0], F32, name=f"bank_{m}{c0}") for m in cuts for c0, c1 in cuts[m]}
-
-        def gather_pass1(j):
-            for a in range(2):
-                lst = offs_t[:, a * HALF // COLS16:(a + 1) * HALF // COLS16]
-                nc.vector.tensor_copy(out=x_il1[a][:, :, j], in_=plane[1, j].indirect(lst))
-
-        gather_pass1(0)
-        gather_pass1(1)
-        for m, z in (("g", 0), ("s", 0), ("h", 0)):
-            round_w(m, z)
-            quant_w(m, z)
-        for m in cuts:
-            for c0, c1 in cuts[m]:
-                mm(bank[m, c0][:], m, 0, c0, c1)
-        gather_pass1(2)
-        gather_pass1(3)
-        round_w("g", 1)
-        quant_w("g", 1)
+            gather_x(0, j)
+        quant_x(0, x_il[0][:], 0, S)
+        for j in range(PACK - 1):
+            gather_x(1, j)
+        round_w("g", 0, nc.scalar.copy, "wil_g0")
+        quant_w("g", 0, "wc_g0")
+        g_banks = banks("g", "first")
+        product("g", g_banks, [0], nc.vector.tensor_copy)
+        gather_x(1, PACK - 1)
+        round_w("g", 1, nc.scalar.copy, "wil_g1")
+        quant_w("g", 1, "wc_g1")
         x_codes.append(keep.tile([P, S], U32, name="xc1", tag="wraw_g1", align_bytes=64))
-        for c0, c1 in cuts["g"]:
-            quant_x(1, x_il1[c0 // HALF][:, c0 % HALF:c0 % HALF + QUARTER, :], c0, c1)
-        for m in ("s", "h"):
-            round_w(m, 1)
-            quant_w(m, 1)
-
-        prod = {
-            "g": keep.tile([P, S], F32, name="g_sb", tag="wraw_h1", align_bytes=64),
-            "s": keep.tile([P, S], F32, name="s_sb", tag="wil_h1", align_bytes=64),
-            "h": keep.tile([P, S], F32, name="h_sb"),
-        }
-        for m in cuts:
-            for c0, c1 in cuts[m]:
-                mm(bank[m, c0][:], m, 1, c0, c1)
-                nc.scalar.copy(out=prod[m][:, c0:c1], in_=bank[m, c0][:])
+        for c0, c1 in cuts:
+            quant_x(1, x_il[1][:, c0:c1, :], c0, c1)
+        for z in range(PASSES):
+            round_w("h", z, nc.scalar.copy, f"wil_h{z}")
+            quant_w("h", z, f"wc_h{z}")
+        product("g", g_banks, [1], nc.vector.tensor_copy)
+        product("h", banks("h", "second"), [0, 1], nc.scalar.copy)
+        round_w("s", 0, nc.scalar.copy, "wil_s0")
+        round_w("s", 1, nc.scalar.copy, "wil_s1")
+        quant_w("s", 0, "ws_g1")
+        s_banks = banks("s", "first")
+        product("s", s_banks, [0], nc.scalar.copy)
+        quant_w("s", 1, "wc_h1")
+        product("s", s_banks, [1], nc.scalar.copy)
 
         gc = keep.tile([P, V], F32, name="gc")
-        sc = keep.tile([P, V], F32, name="sc")
         t1 = keep.tile([P, V], F32, name="t1")
         t2 = keep.tile([P, V], F32, name="t2")
         u1 = keep.tile([P, V], F32, name="u1")
-        u2 = keep.tile([P, V], F32, name="u2")
-        r1 = [keep.tile([P, V // 2], F32, name=f"r1_{a}") for a in range(2)]
-        res = [keep.tile([P, V // 2], F32, name=f"res_{a}") for a in range(2)]
+        ends = [(0, V // 2), (V // 2, V)]
+        r1 = [keep.tile([P, v1 - v0], F32, name=f"r1_{v0}") for v0, v1 in ends]
+        u2 = [keep.tile([P, v1 - v0], F32, name=f"u2_{v0}") for v0, v1 in ends]
+        res = [keep.tile([P, v1 - v0], F32, name=f"res_{v0}") for v0, v1 in ends]
 
         nc.vector.tensor_copy(out=gc[:], in_=prod["g"][:].indirect(cen_t[:]))
-        nc.vector.tensor_copy(out=sc[:], in_=prod["s"][:].indirect(cen_t[:]))
         nc.vector.tensor_tensor(t1[:], prod["h"][:].indirect(pos1_t[:]), gc[:], ALU.mult)
         nc.vector.tensor_tensor(t2[:], prod["h"][:].indirect(pos2_t[:]), gc[:], ALU.mult)
-        nc.vector.tensor_tensor(u1[:], t1[:], sc[:], ALU.add)
-        nc.vector.tensor_tensor(u2[:], t2[:], sc[:], ALU.add)
-        halves = [slice(0, V // 2), slice(V // 2, V)]
-        for a in range(2):
-            nc.scalar.activation(out=r1[a][:], in_=u1[:, halves[a]], func=ACT.Relu)
-        for a in range(2):
-            nc.vector.scalar_tensor_tensor(out=res[a][:], in0=u2[:, halves[a]], scalar=0.0, in1=r1[a][:], op0=ALU.max, op1=ALU.add)
-            nc.sync.dma_start(out=out[:, halves[a]], in_=res[a][:])
+        nc.vector.tensor_tensor(u1[:], prod["s"][:].indirect(cen_t[:]), t1[:], ALU.add)
+        for a, (v0, v1) in enumerate(ends):
+            nc.scalar.activation(out=r1[a][:], in_=u1[:, v0:v1], func=ACT.Relu)
+            nc.vector.tensor_tensor(u2[a][:], prod["s"][:].indirect(cen_t[:, v0 // COLS16:v1 // COLS16]), t2[:, v0:v1], ALU.add)
+        for a, (v0, v1) in enumerate(ends):
+            nc.vector.scalar_tensor_tensor(out=res[a][:], in0=u2[a][:], scalar=0.0, in1=r1[a][:], op0=ALU.max, op1=ALU.add)
+            nc.sync.dma_start(out=out[:, v0:v1], in_=res[a][:])

@@ -53,10 +53,10 @@ def tile_picked_filmg_relu_e_kernel(tc, xT, w1, w2, w3, offs, cen, pos1, pos2, o
 
         load_x(0)
         nc.sync.dma_start(offs_t[:], offs)
-        for q in range(1, 5):
-            load_x(q)
+        load_x(1)
         load_w("g", 0)
-        load_x(5)
+        for q in range(2, len(loads)):
+            load_x(q)
         for m, z in (("g", 1), ("h", 0), ("h", 1), ("s", 0), ("s", 1)):
             load_w(m, z)
         nc.sync.dma_start(cen_t[:], cen)
@@ -119,13 +119,12 @@ def tile_picked_filmg_relu_e_kernel(tc, xT, w1, w2, w3, offs, cen, pos1, pos2, o
         for j in range(PACK):
             gather_x(0, j)
         quant_x(0, x_il[0][:], 0, S)
-        for j in range(PACK - 1):
-            gather_x(1, j)
         round_w("g", 0, nc.scalar.copy, "wil_g0")
         quant_w("g", 0, "wc_g0")
         g_banks = banks("g", "first")
         product("g", g_banks, [0], nc.vector.tensor_copy)
-        gather_x(1, PACK - 1)
+        for j in range(PACK):
+            gather_x(1, j)
         round_w("g", 1, nc.scalar.copy, "wil_g1")
         quant_w("g", 1, "wc_g1")
         x_codes.append(keep.tile([P, S], U32, name="xc1", tag="wraw_g1", align_bytes=64))

@@ -18,6 +18,7 @@ P = 128
 PACK = 4
 K_PASS = P * PACK
 PASSES = K // K_PASS
+HALF = S // 2
 QUARTER = S // 4
 COLS16 = 16
 
@@ -34,7 +35,7 @@ def tile_picked_filmg_relu_e_kernel(tc, xT, w1, w2, w3, offs, cen, pos1, pos2, o
         pos2_t = keep.tile([P, V // COLS16], U16, name="pos2_t")
 
         x_rows = xT.rearrange("(z p j) t -> z p j t", z=PASSES, j=PACK)
-        loads = [(0, 0, 2), (0, 2, 2), (1, 0, 1), (1, 1, 1), (1, 2, 1), (1, 3, 1)]
+        loads = [(0, 0, 2), (0, 2, 1), (0, 3, 1), (1, 0, 1), (1, 1, 1), (1, 2, 1), (1, 3, 1)]
         x_tiles = [keep.tile([P, n, T], F32, name=f"x{z}{j}") for z, j, n in loads]
         plane = {(z, j + i): x_tiles[q][:, i, :] for q, (z, j, n) in enumerate(loads) for i in range(n)}
         weights = {"g": w1, "s": w2, "h": w3}
@@ -53,11 +54,9 @@ def tile_picked_filmg_relu_e_kernel(tc, xT, w1, w2, w3, offs, cen, pos1, pos2, o
 
         load_x(0)
         nc.sync.dma_start(offs_t[:], offs)
-        load_x(1)
-        load_w("g", 0)
-        for q in range(2, len(loads)):
+        for q in range(1, len(loads)):
             load_x(q)
-        for m, z in (("g", 1), ("h", 0), ("h", 1), ("s", 0), ("s", 1)):
+        for m, z in (("g", 0), ("g", 1), ("h", 0), ("h", 1), ("s", 0), ("s", 1)):
             load_w(m, z)
         nc.sync.dma_start(cen_t[:], cen)
         nc.sync.dma_start(pos1_t[:], pos1)
@@ -78,13 +77,17 @@ def tile_picked_filmg_relu_e_kernel(tc, xT, w1, w2, w3, offs, cen, pos1, pos2, o
                 in_=w_il[m, z][:].rearrange("p c j -> p (c j)"),
             )
 
-        x_codes = [keep.tile([P, S], U32, name="xc0", align_bytes=64)]
+        x_codes = {}
         x_scales = [keep.tile([P, S], U8, name=f"xs{z}", align_bytes=64) for z in range(PASSES)]
         x_il = [keep.tile([P, S, PACK], BF16, name=f"xil{z}", align_bytes=64) for z in range(PASSES)]
 
+        def codes_of(z, c0, c1):
+            first = 0 if z == 0 else c0 // HALF * HALF
+            return x_codes[z, first][:, c0 - first:c1 - first]
+
         def quant_x(z, src, c0, c1):
             nc.vector.quantize_mx(
-                out=x_codes[z][:, c0:c1].bitcast(FP8X4),
+                out=codes_of(z, c0, c1).bitcast(FP8X4),
                 scales=x_scales[z][:, c0:c1],
                 in_=src.rearrange("p c j -> p (c j)"),
             )
@@ -94,7 +97,7 @@ def tile_picked_filmg_relu_e_kernel(tc, xT, w1, w2, w3, offs, cen, pos1, pos2, o
                 out=bank,
                 lhsT=w_codes[m, z][:].bitcast(FP8X4),
                 lhsT_scale=w_scales[m, z][:],
-                rhs=x_codes[z][:, c0:c1].bitcast(FP8X4),
+                rhs=codes_of(z, c0, c1).bitcast(FP8X4),
                 rhs_scale=x_scales[z][:, c0:c1],
                 start=(z == 0),
                 stop=(z == PASSES - 1),
@@ -109,39 +112,43 @@ def tile_picked_filmg_relu_e_kernel(tc, xT, w1, w2, w3, offs, cen, pos1, pos2, o
         def banks(m, tag):
             return {c0: psum.tile([P, QUARTER], F32, name=f"bank_{m}{c0}", tag=f"{tag}{c0}") for c0, c1 in cuts}
 
-        def product(m, bank, passes, copy):
-            for c0, c1 in cuts:
+        def product(m, bank, passes, copies):
+            for (c0, c1), copy in zip(cuts, copies):
                 for z in passes:
                     mm(bank[c0][:], m, z, c0, c1)
                 if PASSES - 1 in passes:
                     copy(out=prod[m][:, c0:c1], in_=bank[c0][:])
 
+        g_copies = [nc.vector.tensor_copy] * 4
+        h_copies = [nc.vector.tensor_copy] + [nc.scalar.copy] * 3
+        s_copies = [nc.scalar.copy] * 4
+
         for j in range(PACK):
             gather_x(0, j)
+        x_codes[0, 0] = keep.tile([P, S], U32, name="xc0", align_bytes=64)
         quant_x(0, x_il[0][:], 0, S)
-        round_w("g", 0, nc.scalar.copy, "wil_g0")
-        quant_w("g", 0, "wc_g0")
-        g_banks = banks("g", "first")
-        product("g", g_banks, [0], nc.vector.tensor_copy)
         for j in range(PACK):
             gather_x(1, j)
-        round_w("g", 1, nc.scalar.copy, "wil_g1")
-        quant_w("g", 1, "wc_g1")
-        x_codes.append(keep.tile([P, S], U32, name="xc1", tag="wraw_g1", align_bytes=64))
-        for c0, c1 in cuts:
-            quant_x(1, x_il[1][:, c0:c1, :], c0, c1)
+        g_banks = banks("g", "first")
+        for z in range(PASSES):
+            round_w("g", z, nc.scalar.copy, f"wil_g{z}")
+            quant_w("g", z, f"wc_g{z}")
+            x_codes[1, z * HALF] = keep.tile([P, HALF], U32, name=f"xc1_{z}", tag=f"wraw_g{z}", align_bytes=64)
+            for c0, c1 in cuts[2 * z:2 * z + 2]:
+                quant_x(1, x_il[1][:, c0:c1, :], c0, c1)
+        product("g", g_banks, [0], g_copies)
         for z in range(PASSES):
             round_w("h", z, nc.scalar.copy, f"wil_h{z}")
             quant_w("h", z, f"wc_h{z}")
-        product("g", g_banks, [1], nc.vector.tensor_copy)
-        product("h", banks("h", "second"), [0, 1], nc.scalar.copy)
+        product("g", g_banks, [1], g_copies)
+        product("h", banks("h", "second"), [0, 1], h_copies)
         round_w("s", 0, nc.scalar.copy, "wil_s0")
         round_w("s", 1, nc.scalar.copy, "wil_s1")
         quant_w("s", 0, "ws_g1")
         s_banks = banks("s", "first")
-        product("s", s_banks, [0], nc.scalar.copy)
+        product("s", s_banks, [0], s_copies)
         quant_w("s", 1, "wc_h1")
-        product("s", s_banks, [1], nc.scalar.copy)
+        product("s", s_banks, [1], s_copies)
 
         gc = keep.tile([P, V], F32, name="gc")
         t1 = keep.tile([P, V], F32, name="t1")

@@ -62,12 +62,15 @@ def tile_picked_filmg_relu_e_kernel(tc, xT, w1, w2, w3, offs, cen, pos1, pos2, o
         nc.sync.dma_start(pos1_t[:], pos1)
         nc.sync.dma_start(pos2_t[:], pos2)
 
-        def round_w(m, z, copy, tag):
+        def round_w(m, z, copies, tag):
             w_il[m, z] = keep.tile([P, N, PACK], BF16, name=f"wil_{m}{z}", tag=tag, align_bytes=64)
-            copy(
-                out=w_il[m, z][:].rearrange("p (c i) j -> p c j i", i=4),
-                in_=w_raw[m, z][:].rearrange("p j (c i) -> p c j i", i=4),
-            )
+            width = N // len(copies)
+            for a, copy in enumerate(copies):
+                cols = slice(a * width, (a + 1) * width)
+                copy(
+                    out=w_il[m, z][:, cols, :].rearrange("p (c i) j -> p c j i", i=4),
+                    in_=w_raw[m, z][:, :, cols].rearrange("p j (c i) -> p c j i", i=4),
+                )
 
         def quant_w(m, z, tag):
             w_codes[m, z] = keep.tile([P, N], U32, name=f"wc_{m}{z}", tag=tag, align_bytes=64)
@@ -120,7 +123,7 @@ def tile_picked_filmg_relu_e_kernel(tc, xT, w1, w2, w3, offs, cen, pos1, pos2, o
                     copy(out=prod[m][:, c0:c1], in_=bank[c0][:])
 
         g_copies = [nc.vector.tensor_copy] * 4
-        h_copies = [nc.vector.tensor_copy] + [nc.scalar.copy] * 3
+        h_copies = [nc.scalar.copy] * 4
         s_copies = [nc.scalar.copy] * 4
 
         for j in range(PACK):
@@ -131,19 +134,19 @@ def tile_picked_filmg_relu_e_kernel(tc, xT, w1, w2, w3, offs, cen, pos1, pos2, o
             gather_x(1, j)
         g_banks = banks("g", "first")
         for z in range(PASSES):
-            round_w("g", z, nc.scalar.copy, f"wil_g{z}")
+            round_w("g", z, [nc.scalar.copy], f"wil_g{z}")
             quant_w("g", z, f"wc_g{z}")
             x_codes[1, z * HALF] = keep.tile([P, HALF], U32, name=f"xc1_{z}", tag=f"wraw_g{z}", align_bytes=64)
             for c0, c1 in cuts[2 * z:2 * z + 2]:
                 quant_x(1, x_il[1][:, c0:c1, :], c0, c1)
         product("g", g_banks, [0], g_copies)
         for z in range(PASSES):
-            round_w("h", z, nc.scalar.copy, f"wil_h{z}")
+            round_w("h", z, [nc.scalar.copy], f"wil_h{z}")
             quant_w("h", z, f"wc_h{z}")
         product("g", g_banks, [1], g_copies)
         product("h", banks("h", "second"), [0, 1], h_copies)
-        round_w("s", 0, nc.scalar.copy, "wil_s0")
-        round_w("s", 1, nc.scalar.copy, "wil_s1")
+        round_w("s", 0, [nc.scalar.copy], "wil_s0")
+        round_w("s", 1, [nc.scalar.copy, nc.vector.tensor_copy], "wc_g1")
         quant_w("s", 0, "ws_g1")
         s_banks = banks("s", "first")
         product("s", s_banks, [0], s_copies)

@@ -39,7 +39,9 @@ def tile_picked_filmg_relu_e_kernel(tc, xT, w1, w2, w3, offs, cen, pos1, pos2, o
         x_tiles = [keep.tile([P, n, T], F32, name=f"x{z}{j}") for z, j, n in loads]
         plane = {(z, j + i): x_tiles[q][:, i, :] for q, (z, j, n) in enumerate(loads) for i in range(n)}
         weights = {"g": w1, "s": w2, "h": w3}
-        w_raw = {(m, z): keep.tile([P, PACK, N], F32, name=f"wraw_{m}{z}", tag=f"wraw_{m}{z}", align_bytes=64) for m in weights for z in range(PASSES)}
+        lead = {("h", 0): N, ("h", 1): 3 * N // 2}
+        w_home = {(m, z): keep.tile([P, lead.get((m, z), 0) + PACK * N], F32, name=f"wraw_{m}{z}", tag=f"wraw_{m}{z}", align_bytes=64) for m in weights for z in range(PASSES)}
+        w_raw = {key: home[:, lead.get(key, 0):].rearrange("p (j c) -> p j c", j=PACK) for key, home in w_home.items()}
         w_il = {}
         w_codes = {}
         w_scales = {(m, z): keep.tile([P, N], U8, name=f"ws_{m}{z}", tag=f"ws_{m}{z}", align_bytes=64) for m in weights for z in range(PASSES)}
@@ -50,20 +52,28 @@ def tile_picked_filmg_relu_e_kernel(tc, xT, w1, w2, w3, offs, cen, pos1, pos2, o
 
         def load_w(m, z):
             rows = weights[m][z * K_PASS:(z + 1) * K_PASS, :]
-            nc.sync.dma_start(out=w_raw[m, z][:], in_=rows.rearrange("(p j) c -> p j c", j=PACK))
+            nc.sync.dma_start(out=w_raw[m, z], in_=rows.rearrange("(p j) c -> p j c", j=PACK))
 
         load_x(0)
         nc.sync.dma_start(offs_t[:], offs)
         for q in range(1, len(loads)):
             load_x(q)
-        for m, z in (("g", 0), ("g", 1), ("h", 0), ("h", 1), ("s", 0), ("s", 1)):
+        for m, z in (("g", 0), ("g", 1), ("h", 0), ("h", 1)):
             load_w(m, z)
         nc.sync.dma_start(cen_t[:], cen)
+        for z in range(PASSES):
+            load_w("s", z)
         nc.sync.dma_start(pos1_t[:], pos1)
         nc.sync.dma_start(pos2_t[:], pos2)
 
-        def round_w(m, z, copies, tag):
-            w_il[m, z] = keep.tile([P, N, PACK], BF16, name=f"wil_{m}{z}", tag=tag, align_bytes=64)
+        def own(name, tag):
+            return keep.tile([P, N * PACK], BF16, name=name, tag=tag, align_bytes=64)[:]
+
+        def ahead_of(key):
+            return w_home[key][:, :N * PACK // 2].bitcast(BF16)
+
+        def round_w(m, z, copies, place):
+            w_il[m, z] = place.rearrange("p (c j) -> p c j", j=PACK)
             width = N // len(copies)
             for a, copy in enumerate(copies):
                 cols = slice(a * width, (a + 1) * width)
@@ -77,7 +87,7 @@ def tile_picked_filmg_relu_e_kernel(tc, xT, w1, w2, w3, offs, cen, pos1, pos2, o
             nc.vector.quantize_mx(
                 out=w_codes[m, z][:].bitcast(FP8X4),
                 scales=w_scales[m, z][:],
-                in_=w_il[m, z][:].rearrange("p c j -> p (c j)"),
+                in_=w_il[m, z].rearrange("p c j -> p (c j)"),
             )
 
         x_codes = {}
@@ -110,21 +120,19 @@ def tile_picked_filmg_relu_e_kernel(tc, xT, w1, w2, w3, offs, cen, pos1, pos2, o
             nc.vector.tensor_copy(out=x_il[z][:, :, j], in_=plane[z, j].indirect(offs_t[:]))
 
         cuts = [(c, c + QUARTER) for c in range(0, S, QUARTER)]
-        prod = {m: keep.tile([P, S], F32, name=f"{m}_sb") for m in weights}
+        prod = {}
 
         def banks(m, tag):
             return {c0: psum.tile([P, QUARTER], F32, name=f"bank_{m}{c0}", tag=f"{tag}{c0}") for c0, c1 in cuts}
 
-        def product(m, bank, passes, copies):
-            for (c0, c1), copy in zip(cuts, copies):
-                for z in passes:
-                    mm(bank[c0][:], m, z, c0, c1)
-                if PASSES - 1 in passes:
-                    copy(out=prod[m][:, c0:c1], in_=bank[c0][:])
+        def product(m, bank, z):
+            for c0, c1 in cuts:
+                mm(bank[c0][:], m, z, c0, c1)
 
-        g_copies = [nc.vector.tensor_copy] * 4
-        h_copies = [nc.scalar.copy] * 4
-        s_copies = [nc.scalar.copy] * 4
+        def leave_psum(m, bank, tag):
+            prod[m] = keep.tile([P, S], F32, name=f"{m}_sb", tag=tag, align_bytes=64)
+            for c0, c1 in cuts:
+                nc.scalar.copy(out=prod[m][:, c0:c1], in_=bank[c0][:])
 
         for j in range(PACK):
             gather_x(0, j)
@@ -134,41 +142,50 @@ def tile_picked_filmg_relu_e_kernel(tc, xT, w1, w2, w3, offs, cen, pos1, pos2, o
             gather_x(1, j)
         g_banks = banks("g", "first")
         for z in range(PASSES):
-            round_w("g", z, [nc.scalar.copy], f"wil_g{z}")
+            round_w("g", z, [nc.scalar.copy], own(f"wil_g{z}", f"wil_g{z}"))
             quant_w("g", z, f"wc_g{z}")
             x_codes[1, z * HALF] = keep.tile([P, HALF], U32, name=f"xc1_{z}", tag=f"wraw_g{z}", align_bytes=64)
-            for c0, c1 in cuts[2 * z:2 * z + 2]:
-                quant_x(1, x_il[1][:, c0:c1, :], c0, c1)
-        product("g", g_banks, [0], g_copies)
+            quant_x(1, x_il[1][:, z * HALF:(z + 1) * HALF, :], z * HALF, (z + 1) * HALF)
         for z in range(PASSES):
-            round_w("h", z, [nc.scalar.copy], f"wil_h{z}")
+            product("g", g_banks, z)
+        round_w("h", 0, [nc.scalar.copy], own("wil_h0", "wil_h0"))
+        round_w("h", 1, [nc.scalar.copy, nc.vector.tensor_copy], ahead_of(("h", 0)))
+        h_banks = banks("h", "second")
+        for z in range(PASSES):
             quant_w("h", z, f"wc_h{z}")
-        product("g", g_banks, [1], g_copies)
-        product("h", banks("h", "second"), [0, 1], h_copies)
-        round_w("s", 0, [nc.scalar.copy], "wil_s0")
-        round_w("s", 1, [nc.scalar.copy, nc.vector.tensor_copy], "wc_g1")
-        quant_w("s", 0, "ws_g1")
+            product("h", h_banks, z)
+        leave_psum("g", g_banks, "g_sb")
+        gc_home = keep.tile([P, V + V // 2], F32, name="gc_home")
+        gc = gc_home[:, V // 2:]
+        nc.vector.tensor_copy(out=gc, in_=prod["g"][:].indirect(cen_t[:]))
+        round_w("s", 0, [nc.vector.tensor_copy], ahead_of(("h", 1)))
+        round_w("s", 1, [nc.scalar.copy, nc.vector.tensor_copy], ahead_of(("h", 0)))
+        leave_psum("h", h_banks, "h_sb")
         s_banks = banks("s", "first")
-        product("s", s_banks, [0], s_copies)
-        quant_w("s", 1, "wc_h1")
-        product("s", s_banks, [1], s_copies)
+        for z in range(PASSES):
+            quant_w("s", z, f"wc_s{z}")
+            product("s", s_banks, z)
+        leave_psum("s", s_banks, "s_sb")
 
-        gc = keep.tile([P, V], F32, name="gc")
         t1 = keep.tile([P, V], F32, name="t1")
         t2 = keep.tile([P, V], F32, name="t2")
-        u1 = keep.tile([P, V], F32, name="u1")
-        ends = [(0, V // 2), (V // 2, V)]
-        r1 = [keep.tile([P, v1 - v0], F32, name=f"r1_{v0}") for v0, v1 in ends]
-        u2 = [keep.tile([P, v1 - v0], F32, name=f"u2_{v0}") for v0, v1 in ends]
-        res = [keep.tile([P, v1 - v0], F32, name=f"res_{v0}") for v0, v1 in ends]
+        r1 = keep.tile([P, V], F32, name="r1")
+        u2 = keep.tile([P, V], F32, name="u2")
+        res = keep.tile([P, V], F32, name="res")
+        ends = [slice(0, V // 2), slice(V // 2, V)]
 
-        nc.vector.tensor_copy(out=gc[:], in_=prod["g"][:].indirect(cen_t[:]))
-        nc.vector.tensor_tensor(t1[:], prod["h"][:].indirect(pos1_t[:]), gc[:], ALU.mult)
-        nc.vector.tensor_tensor(t2[:], prod["h"][:].indirect(pos2_t[:]), gc[:], ALU.mult)
-        nc.vector.tensor_tensor(u1[:], prod["s"][:].indirect(cen_t[:]), t1[:], ALU.add)
-        for a, (v0, v1) in enumerate(ends):
-            nc.scalar.activation(out=r1[a][:], in_=u1[:, v0:v1], func=ACT.Relu)
-            nc.vector.tensor_tensor(u2[a][:], prod["s"][:].indirect(cen_t[:, v0 // COLS16:v1 // COLS16]), t2[:, v0:v1], ALU.add)
-        for a, (v0, v1) in enumerate(ends):
-            nc.vector.scalar_tensor_tensor(out=res[a][:], in0=u2[a][:], scalar=0.0, in1=r1[a][:], op0=ALU.max, op1=ALU.add)
-            nc.sync.dma_start(out=out[:, v0:v1], in_=res[a][:])
+        def picked(m, places, v):
+            return prod[m][:].indirect(places[:, v.start // COLS16:v.stop // COLS16])
+
+        nc.vector.tensor_tensor(t1[:], prod["h"][:].indirect(pos1_t[:]), gc, ALU.mult)
+        for v in ends:
+            nc.vector.tensor_tensor(t2[:, v], picked("h", pos2_t, v), gc[:, v], ALU.mult)
+        u1 = gc_home[:, :V]
+        nc.vector.tensor_tensor(u1, prod["s"][:].indirect(cen_t[:]), t1[:], ALU.add)
+        for v in ends:
+            nc.scalar.activation(out=r1[:, v], in_=u1[:, v], func=ACT.Relu)
+        for v in ends:
+            nc.vector.tensor_tensor(u2[:, v], picked("s", cen_t, v), t2[:, v], ALU.add)
+        for v in ends:
+            nc.vector.scalar_tensor_tensor(out=res[:, v], in0=u2[:, v], scalar=0.0, in1=r1[:, v], op0=ALU.max, op1=ALU.add)
+            nc.sync.dma_start(out=out[:, v], in_=res[:, v])

@@ -27,6 +27,7 @@ def tile_picked_filmg_relu_e_kernel(tc, xT, w1, w2, w3, offs, cen, pos1, pos2, o
     nc = tc.nc
     with ExitStack() as ctx:
         keep = ctx.enter_context(tc.tile_pool(name="keep", bufs=1))
+        laid = ctx.enter_context(tc.tile_pool(name="laid", bufs=1))
         psum = ctx.enter_context(tc.psum_pool(name="psum", bufs=1))
 
         offs_t = keep.tile([P, S // COLS16], U16, name="offs_t")
@@ -35,157 +36,164 @@ def tile_picked_filmg_relu_e_kernel(tc, xT, w1, w2, w3, offs, cen, pos1, pos2, o
         pos2_t = keep.tile([P, V // COLS16], U16, name="pos2_t")
 
         x_rows = xT.rearrange("(z p j) t -> z p j t", z=PASSES, j=PACK)
-        loads = [(0, 0, 2), (0, 2, 1), (0, 3, 1), (1, 0, 1), (1, 1, 1), (1, 2, 1), (1, 3, 1)]
-        x_tiles = [keep.tile([P, n, T], F32, name=f"x{z}{j}") for z, j, n in loads]
-        plane = {(z, j + i): x_tiles[q][:, i, :] for q, (z, j, n) in enumerate(loads) for i in range(n)}
         weights = {"g": w1, "s": w2, "h": w3}
-        lead = {("h", 0): N, ("h", 1): 3 * N // 2}
-        w_home = {(m, z): keep.tile([P, lead.get((m, z), 0) + PACK * N], F32, name=f"wraw_{m}{z}", tag=f"wraw_{m}{z}", align_bytes=64) for m in weights for z in range(PASSES)}
-        w_raw = {key: home[:, lead.get(key, 0):].rearrange("p (j c) -> p j c", j=PACK) for key, home in w_home.items()}
-        w_il = {}
-        w_codes = {}
-        w_scales = {(m, z): keep.tile([P, N], U8, name=f"ws_{m}{z}", tag=f"ws_{m}{z}", align_bytes=64) for m in weights for z in range(PASSES)}
+        plane = {}
+        w_raw = {}
 
-        def load_x(q):
-            z, j, n = loads[q]
-            nc.sync.dma_start(out=x_tiles[q][:], in_=x_rows[z, :, j:j + n, :])
+        def load_x(z, j, n):
+            if (z, j) == (1, 2):
+                rows = laid.tile([P, n, T], F32, name="x12", offset=0, align_bytes=64)
+            else:
+                rows = keep.tile([P, n, T], F32, name=f"x{z}{j}")
+            nc.sync.dma_start(out=rows[:], in_=x_rows[z, :, j:j + n, :])
+            for i in range(n):
+                plane[z, j + i] = rows[:, i, :]
 
         def load_w(m, z):
+            if (m, z) == ("h", 1):
+                w_raw[m, z] = laid.tile([P, PACK, N], F32, name="wraw_h1", offset=4 * T, align_bytes=64)
+            else:
+                w_raw[m, z] = keep.tile([P, PACK, N], F32, name=f"wraw_{m}{z}", tag=f"wraw_{m}{z}", align_bytes=64)
             rows = weights[m][z * K_PASS:(z + 1) * K_PASS, :]
-            nc.sync.dma_start(out=w_raw[m, z], in_=rows.rearrange("(p j) c -> p j c", j=PACK))
+            nc.sync.dma_start(out=w_raw[m, z][:], in_=rows.rearrange("(p j) c -> p j c", j=PACK))
 
-        load_x(0)
+        load_x(0, 0, 2)
         nc.sync.dma_start(offs_t[:], offs)
-        for q in range(1, len(loads)):
-            load_x(q)
-        for m, z in (("g", 0), ("g", 1), ("h", 0), ("h", 1)):
-            load_w(m, z)
+        load_x(0, 2, 2)
+        load_w("g", 0)
+        load_w("h", 0)
+        for j in range(PACK):
+            load_x(1, j, 1)
+        load_w("g", 1)
+        load_w("h", 1)
+        load_w("s", 0)
+        load_w("s", 1)
         nc.sync.dma_start(cen_t[:], cen)
-        for z in range(PASSES):
-            load_w("s", z)
         nc.sync.dma_start(pos1_t[:], pos1)
         nc.sync.dma_start(pos2_t[:], pos2)
 
-        def own(name, tag):
-            return keep.tile([P, N * PACK], BF16, name=name, tag=tag, align_bytes=64)[:]
+        w_codes = {}
+        w_scales = {}
 
-        def ahead_of(key):
-            return w_home[key][:, :N * PACK // 2].bitcast(BF16)
+        def rounded_tile(pieces, tag):
+            return keep.tile([P, len(pieces), N, PACK], BF16, name="wil_" + tag, tag=tag, align_bytes=64)
 
-        def round_w(m, z, copies, place):
-            w_il[m, z] = place.rearrange("p (c j) -> p c j", j=PACK)
-            width = N // len(copies)
-            for a, copy in enumerate(copies):
-                cols = slice(a * width, (a + 1) * width)
-                copy(
-                    out=w_il[m, z][:, cols, :].rearrange("p (c i) j -> p c j i", i=4),
-                    in_=w_raw[m, z][:, :, cols].rearrange("p j (c i) -> p c j i", i=4),
-                )
-
-        def quant_w(m, z, tag):
-            w_codes[m, z] = keep.tile([P, N], U32, name=f"wc_{m}{z}", tag=tag, align_bytes=64)
-            nc.vector.quantize_mx(
-                out=w_codes[m, z][:].bitcast(FP8X4),
-                scales=w_scales[m, z][:],
-                in_=w_il[m, z].rearrange("p c j -> p (c j)"),
+        def round_w(piece, copy, place):
+            copy(
+                out=place.rearrange("p (c i) j -> p c j i", i=4),
+                in_=w_raw[piece][:].rearrange("p j (c i) -> p c j i", i=4),
             )
+
+        def quant_w(pieces, rounded, tag):
+            if len(pieces) > 1:
+                codes = laid.tile([P, len(pieces) * N], U32, name="wc_" + tag, offset=4 * S, align_bytes=64)
+            else:
+                codes = keep.tile([P, len(pieces) * N], U32, name="wc_" + tag, tag=tag, align_bytes=64)
+            scales = keep.tile([P, len(pieces) * N], U8, name="ws_" + tag, align_bytes=64)
+            nc.vector.quantize_mx(out=codes[:].bitcast(FP8X4), scales=scales[:], in_=rounded[:].rearrange("p a c j -> p (a c j)"))
+            for a, piece in enumerate(pieces):
+                w_codes[piece] = codes[:, a * N:(a + 1) * N]
+                w_scales[piece] = scales[:, a * N:(a + 1) * N]
+
+        def prepare_w(pieces, copy, rounded_tag, codes_tag):
+            rounded = rounded_tile(pieces, rounded_tag)
+            for a, piece in enumerate(pieces):
+                round_w(piece, copy, rounded[:, a, :, :])
+            quant_w(pieces, rounded, codes_tag)
 
         x_codes = {}
         x_scales = [keep.tile([P, S], U8, name=f"xs{z}", align_bytes=64) for z in range(PASSES)]
         x_il = [keep.tile([P, S, PACK], BF16, name=f"xil{z}", align_bytes=64) for z in range(PASSES)]
 
-        def codes_of(z, c0, c1):
-            first = 0 if z == 0 else c0 // HALF * HALF
-            return x_codes[z, first][:, c0 - first:c1 - first]
-
-        def quant_x(z, src, c0, c1):
-            nc.vector.quantize_mx(
-                out=codes_of(z, c0, c1).bitcast(FP8X4),
-                scales=x_scales[z][:, c0:c1],
-                in_=src.rearrange("p c j -> p (c j)"),
-            )
-
-        def mm(bank, m, z, c0, c1):
-            nc.tensor.matmul_mx(
-                out=bank,
-                lhsT=w_codes[m, z][:].bitcast(FP8X4),
-                lhsT_scale=w_scales[m, z][:],
-                rhs=codes_of(z, c0, c1).bitcast(FP8X4),
-                rhs_scale=x_scales[z][:, c0:c1],
-                start=(z == 0),
-                stop=(z == PASSES - 1),
-            )
-
         def gather_x(z, j):
-            nc.vector.tensor_copy(out=x_il[z][:, :, j], in_=plane[z, j].indirect(offs_t[:]))
+            nc.vector.tensor_copy(out=x_il[z][:, :HALF, j], in_=plane[z, j].indirect(offs_t[:, :HALF // COLS16]))
+            rest = keep.tile([P, HALF], F32, name=f"rest{z}{j}")
+            nc.scalar.activation(out=rest[:], in_=plane[z, j].indirect(offs_t[:, HALF // COLS16:]), func=ACT.Copy)
+            nc.vector.tensor_copy(out=x_il[z][:, HALF:, j], in_=rest[:])
 
-        cuts = [(c, c + QUARTER) for c in range(0, S, QUARTER)]
+        def quant_x(z, c0, codes, width):
+            for c in range(0, codes.shape[1], QUARTER):
+                x_codes[z, c0 + c] = codes[:, c:]
+            for c in range(0, codes.shape[1], width):
+                nc.vector.quantize_mx(
+                    out=codes[:, c:c + width].bitcast(FP8X4),
+                    scales=x_scales[z][:, c0 + c:c0 + c + width],
+                    in_=x_il[z][:, c0 + c:c0 + c + width, :].rearrange("p c j -> p (c j)"),
+                )
+
+        cut = {"g": QUARTER, "h": HALF, "s": HALF}
+        banks = {(m, c): psum.tile([P, cut[m]], F32, name=f"bank_{m}{c}") for m in cut for c in range(0, S, cut[m])}
         prod = {}
 
-        def banks(m, tag):
-            return {c0: psum.tile([P, QUARTER], F32, name=f"bank_{m}{c0}", tag=f"{tag}{c0}") for c0, c1 in cuts}
+        def product(m, z, c0, c1):
+            for c in range(c0, c1, cut[m]):
+                nc.tensor.matmul_mx(
+                    out=banks[m, c][:],
+                    lhsT=w_codes[m, z].bitcast(FP8X4),
+                    lhsT_scale=w_scales[m, z],
+                    rhs=x_codes[z, c][:, :cut[m]].bitcast(FP8X4),
+                    rhs_scale=x_scales[z][:, c:c + cut[m]],
+                    start=(z == 0),
+                    stop=(z == PASSES - 1),
+                )
 
-        def product(m, bank, z):
-            for c0, c1 in cuts:
-                mm(bank[c0][:], m, z, c0, c1)
-
-        def leave_psum(m, bank, tag):
+        def leave_psum(m, tag):
             prod[m] = keep.tile([P, S], F32, name=f"{m}_sb", tag=tag, align_bytes=64)
-            for c0, c1 in cuts:
-                nc.scalar.copy(out=prod[m][:, c0:c1], in_=bank[c0][:])
+            for c in range(0, S, cut[m]):
+                nc.scalar.copy(out=prod[m][:, c:c + cut[m]], in_=banks[m, c][:])
 
         for j in range(PACK):
             gather_x(0, j)
-        x_codes[0, 0] = keep.tile([P, S], U32, name="xc0", align_bytes=64)
-        quant_x(0, x_il[0][:], 0, S)
-        for j in range(PACK):
+        for j in range(PACK - 1):
             gather_x(1, j)
-        g_banks = banks("g", "first")
+        quant_x(0, 0, laid.tile([P, S], U32, name="xc0", offset=0, align_bytes=64), S)
+        prepare_w([("g", 0), ("h", 0)], nc.scalar.copy, "r_gh0", "c_gh0")
+        product("g", 0, 0, S)
+        product("h", 0, 0, S)
+        gather_x(1, PACK - 1)
+        prepare_w([("g", 1)], nc.scalar.copy, "r_g1", "c_g1")
+        quant_x(1, 0, keep.tile([P, HALF], U32, name="xc1a", tag="wraw_g1", align_bytes=64), QUARTER)
+        prepare_w([("h", 1)], nc.scalar.copy, "r_h1", "c_h1")
+        quant_x(1, HALF, laid.tile([P, HALF], U32, name="xc1b", offset=4 * T, align_bytes=64), QUARTER)
+        s_rounded = [rounded_tile([("s", 0)], "r_s0"), laid.tile([P, 1, N, PACK], BF16, name="r_s1", offset=4 * T + 4 * HALF, align_bytes=64)]
+        round_w(("s", 0), nc.scalar.copy, s_rounded[0][:, 0, :, :])
+        round_w(("s", 1), nc.vector.tensor_copy, s_rounded[1][:, 0, :, :])
         for z in range(PASSES):
-            round_w("g", z, [nc.scalar.copy], own(f"wil_g{z}", f"wil_g{z}"))
-            quant_w("g", z, f"wc_g{z}")
-            x_codes[1, z * HALF] = keep.tile([P, HALF], U32, name=f"xc1_{z}", tag=f"wraw_g{z}", align_bytes=64)
-            quant_x(1, x_il[1][:, z * HALF:(z + 1) * HALF, :], z * HALF, (z + 1) * HALF)
+            quant_w([("s", z)], s_rounded[z], f"c_s{z}")
+        for c in (0, HALF):
+            product("g", 1, c, c + HALF)
+            product("h", 1, c, c + HALF)
         for z in range(PASSES):
-            product("g", g_banks, z)
-        round_w("h", 0, [nc.scalar.copy], own("wil_h0", "wil_h0"))
-        round_w("h", 1, [nc.scalar.copy, nc.vector.tensor_copy], ahead_of(("h", 0)))
-        h_banks = banks("h", "second")
-        for z in range(PASSES):
-            quant_w("h", z, f"wc_h{z}")
-            product("h", h_banks, z)
-        leave_psum("g", g_banks, "g_sb")
-        gc_home = keep.tile([P, V + V // 2], F32, name="gc_home")
-        gc = gc_home[:, V // 2:]
-        nc.vector.tensor_copy(out=gc, in_=prod["g"][:].indirect(cen_t[:]))
-        round_w("s", 0, [nc.vector.tensor_copy], ahead_of(("h", 1)))
-        round_w("s", 1, [nc.scalar.copy, nc.vector.tensor_copy], ahead_of(("h", 0)))
-        leave_psum("h", h_banks, "h_sb")
-        s_banks = banks("s", "first")
-        for z in range(PASSES):
-            quant_w("s", z, f"wc_s{z}")
-            product("s", s_banks, z)
-        leave_psum("s", s_banks, "s_sb")
+            product("s", z, 0, S)
 
-        t1 = keep.tile([P, V], F32, name="t1")
-        t2 = keep.tile([P, V], F32, name="t2")
-        r1 = keep.tile([P, V], F32, name="r1")
-        u2 = keep.tile([P, V], F32, name="u2")
-        res = keep.tile([P, V], F32, name="res")
         ends = [slice(0, V // 2), slice(V // 2, V)]
 
         def picked(m, places, v):
             return prod[m][:].indirect(places[:, v.start // COLS16:v.stop // COLS16])
 
-        nc.vector.tensor_tensor(t1[:], prod["h"][:].indirect(pos1_t[:]), gc, ALU.mult)
+        leave_psum("g", "wraw_s0")
+        gc = keep.tile([P, V], F32, name="gc", tag="wraw_s1", align_bytes=64)
         for v in ends:
-            nc.vector.tensor_tensor(t2[:, v], picked("h", pos2_t, v), gc[:, v], ALU.mult)
-        u1 = gc_home[:, :V]
-        nc.vector.tensor_tensor(u1, prod["s"][:].indirect(cen_t[:]), t1[:], ALU.add)
+            nc.vector.tensor_copy(out=gc[:, v], in_=picked("g", cen_t, v))
+        leave_psum("h", "r_s0")
+        t1 = keep.tile([P, V], F32, name="t1")
+        t2 = keep.tile([P, V], F32, name="t2")
         for v in ends:
+            nc.vector.tensor_tensor(t1[:, v], picked("h", pos1_t, v), gc[:, v], ALU.mult)
+        nc.vector.tensor_tensor(t2[:], prod["h"][:].indirect(pos2_t[:]), gc[:], ALU.mult)
+        leave_psum("s", "s_sb")
+        sc = keep.tile([P, V], F32, name="sc")
+        nc.scalar.activation(out=sc[:], in_=prod["s"][:].indirect(cen_t[:]), func=ACT.Copy)
+
+        u1 = keep.tile([P, V], F32, name="u1")
+        r1 = keep.tile([P, V], F32, name="r1")
+        u2 = keep.tile([P, V], F32, name="u2")
+        res = keep.tile([P, V], F32, name="res")
+        for v in ends:
+            nc.vector.tensor_tensor(u1[:, v], t1[:, v], sc[:, v], ALU.add)
             nc.scalar.activation(out=r1[:, v], in_=u1[:, v], func=ACT.Relu)
         for v in ends:
-            nc.vector.tensor_tensor(u2[:, v], picked("s", cen_t, v), t2[:, v], ALU.add)
+            nc.vector.tensor_tensor(u2[:, v], t2[:, v], sc[:, v], ALU.add)
         for v in ends:
             nc.vector.scalar_tensor_tensor(out=res[:, v], in0=u2[:, v], scalar=0.0, in1=r1[:, v], op0=ALU.max, op1=ALU.add)
             nc.sync.dma_start(out=out[:, v], in_=res[:, v])

@@ -150,6 +150,15 @@ def tile_picked_filmg_relu_e_kernel(tc, xT, w1, w2, w3, offs, cen, pos1, pos2, o
         prepare_w([("g", 0), ("h", 0)], nc.scalar.copy, "r_gh0", "c_gh0")
         product("g", 0, 0, S)
         product("h", 0, 0, S)
+        nc.tensor.matmul_mx(
+            out=banks["s", 0][:],
+            lhsT=w_codes["h", 0].bitcast(FP8X4),
+            lhsT_scale=w_scales["h", 0],
+            rhs=x_codes[0, 0][:, :HALF].bitcast(FP8X4),
+            rhs_scale=x_scales[0][:, :HALF],
+            start=True,
+            stop=True,
+        )
         gather_x(1, PACK - 1)
         prepare_w([("g", 1)], nc.scalar.copy, "r_g1", "c_g1")
         quant_x(1, 0, keep.tile([P, HALF], U32, name="xc1a", tag="wraw_g1", align_bytes=64), QUARTER)

@@ -57,13 +57,13 @@ def tile_picked_filmg_relu_e_kernel(tc, xT, w1, w2, w3, offs, cen, pos1, pos2, o
             rows = weights[m][z * K_PASS:(z + 1) * K_PASS, :]
             nc.sync.dma_start(out=w_raw[m, z][:], in_=rows.rearrange("(p j) c -> p j c", j=PACK))
 
-        load_x(0, 0, 2)
-        nc.sync.dma_start(offs_t[:], offs)
-        load_x(0, 2, 2)
         load_w("g", 0)
         load_w("h", 0)
-        for j in range(PACK):
-            load_x(1, j, 1)
+        nc.sync.dma_start(offs_t[:], offs)
+        load_x(0, 0, PACK)
+        load_x(1, 0, 2)
+        load_x(1, 2, 1)
+        load_x(1, 3, 1)
         load_w("g", 1)
         load_w("h", 1)
         load_w("s", 0)
@@ -105,11 +105,27 @@ def tile_picked_filmg_relu_e_kernel(tc, xT, w1, w2, w3, offs, cen, pos1, pos2, o
         x_scales = [keep.tile([P, S], U8, name=f"xs{z}", align_bytes=64) for z in range(PASSES)]
         x_il = [keep.tile([P, S, PACK], BF16, name=f"xil{z}", align_bytes=64) for z in range(PASSES)]
 
-        def gather_x(z, j):
-            nc.vector.tensor_copy(out=x_il[z][:, :HALF, j], in_=plane[z, j].indirect(offs_t[:, :HALF // COLS16]))
-            rest = keep.tile([P, HALF], F32, name=f"rest{z}{j}")
-            nc.scalar.activation(out=rest[:], in_=plane[z, j].indirect(offs_t[:, HALF // COLS16:]), func=ACT.Copy)
-            nc.vector.tensor_copy(out=x_il[z][:, HALF:, j], in_=rest[:])
+        def listed(z, j, c):
+            return plane[z, j].indirect(offs_t[:, c // COLS16:(c + HALF) // COLS16])
+
+        def gather_planes(z, j0, n):
+            picked = {c: keep.tile([P, n, HALF], F32, name=f"picked{z}{j0}_{c}") for c in (0, HALF)}
+            for c in picked:
+                for i in range(n // 2):
+                    nc.vector.tensor_copy(out=picked[c][:, i, :], in_=listed(z, j0 + i, c))
+                for i in range(n // 2, n):
+                    nc.scalar.activation(out=picked[c][:, i, :], in_=listed(z, j0 + i, c), func=ACT.Copy)
+            for c in picked:
+                nc.vector.tensor_copy(
+                    out=x_il[z][:, c:c + HALF, j0:j0 + n].rearrange("p (c i) j -> p c j i", i=4),
+                    in_=picked[c][:].rearrange("p j (c i) -> p c j i", i=4),
+                )
+
+        def gather_plane(z, j):
+            picked = keep.tile([P, HALF], F32, name=f"picked{z}{j}")
+            nc.vector.tensor_copy(out=x_il[z][:, :HALF, j], in_=listed(z, j, 0))
+            nc.scalar.activation(out=picked[:], in_=listed(z, j, HALF), func=ACT.Copy)
+            nc.vector.tensor_copy(out=x_il[z][:, HALF:, j], in_=picked[:])
 
         def quant_x(z, c0, codes, width):
             for c in range(0, codes.shape[1], QUARTER):
@@ -142,24 +158,15 @@ def tile_picked_filmg_relu_e_kernel(tc, xT, w1, w2, w3, offs, cen, pos1, pos2, o
             for c in range(0, S, cut[m]):
                 nc.scalar.copy(out=prod[m][:, c:c + cut[m]], in_=banks[m, c][:])
 
-        for j in range(PACK):
-            gather_x(0, j)
-        for j in range(PACK - 1):
-            gather_x(1, j)
-        quant_x(0, 0, laid.tile([P, S], U32, name="xc0", offset=0, align_bytes=64), S)
+        gather_planes(0, 0, PACK)
+        quant_x(0, 0, keep.tile([P, HALF], U32, name="xc0a", align_bytes=64), HALF)
+        gather_planes(1, 0, 2)
+        gather_plane(1, 2)
+        quant_x(0, HALF, laid.tile([P, HALF], U32, name="xc0b", offset=0, align_bytes=64), HALF)
         prepare_w([("g", 0), ("h", 0)], nc.scalar.copy, "r_gh0", "c_gh0")
         product("g", 0, 0, S)
         product("h", 0, 0, S)
-        nc.tensor.matmul_mx(
-            out=banks["s", 0][:],
-            lhsT=w_codes["h", 0].bitcast(FP8X4),
-            lhsT_scale=w_scales["h", 0],
-            rhs=x_codes[0, 0][:, :HALF].bitcast(FP8X4),
-            rhs_scale=x_scales[0][:, :HALF],
-            start=True,
-            stop=True,
-        )
-        gather_x(1, PACK - 1)
+        gather_plane(1, 3)
         prepare_w([("g", 1)], nc.scalar.copy, "r_g1", "c_g1")
         quant_x(1, 0, keep.tile([P, HALF], U32, name="xc1a", tag="wraw_g1", align_bytes=64), QUARTER)
         prepare_w([("h", 1)], nc.scalar.copy, "r_h1", "c_h1")
@@ -177,18 +184,18 @@ def tile_picked_filmg_relu_e_kernel(tc, xT, w1, w2, w3, offs, cen, pos1, pos2, o
 
         ends = [slice(0, V // 2), slice(V // 2, V)]
 
-        def picked(m, places, v):
+        def fetched(m, places, v):
             return prod[m][:].indirect(places[:, v.start // COLS16:v.stop // COLS16])
 
         leave_psum("g", "wraw_s0")
         gc = keep.tile([P, V], F32, name="gc", tag="wraw_s1", align_bytes=64)
         for v in ends:
-            nc.vector.tensor_copy(out=gc[:, v], in_=picked("g", cen_t, v))
+            nc.vector.tensor_copy(out=gc[:, v], in_=fetched("g", cen_t, v))
         leave_psum("h", "r_s0")
         t1 = keep.tile([P, V], F32, name="t1")
         t2 = keep.tile([P, V], F32, name="t2")
         for v in ends:
-            nc.vector.tensor_tensor(t1[:, v], picked("h", pos1_t, v), gc[:, v], ALU.mult)
+            nc.vector.tensor_tensor(t1[:, v], fetched("h", pos1_t, v), gc[:, v], ALU.mult)
         nc.vector.tensor_tensor(t2[:], prod["h"][:].indirect(pos2_t[:]), gc[:], ALU.mult)
         leave_psum("s", "s_sb")
         sc = keep.tile([P, V], F32, name="sc")

@@ -41,80 +41,67 @@ def tile_picked_filmg_relu_e_kernel(tc, xT, w1, w2, w3, offs, cen, pos1, pos2, o
         w_raw = {}
 
         def load_x(z, j, n):
-            if (z, j) == (1, 2):
-                rows = laid.tile([P, n, T], F32, name="x12", offset=0, align_bytes=64)
-            else:
-                rows = keep.tile([P, n, T], F32, name=f"x{z}{j}")
+            rows = keep.tile([P, n, T], F32, name=f"x{z}{j}")
             nc.sync.dma_start(out=rows[:], in_=x_rows[z, :, j:j + n, :])
             for i in range(n):
                 plane[z, j + i] = rows[:, i, :]
 
         def load_w(m, z):
-            if (m, z) == ("h", 1):
-                w_raw[m, z] = laid.tile([P, PACK, N], F32, name="wraw_h1", offset=4 * T, align_bytes=64)
-            else:
-                w_raw[m, z] = keep.tile([P, PACK, N], F32, name=f"wraw_{m}{z}", tag=f"wraw_{m}{z}", align_bytes=64)
+            w_raw[m, z] = keep.tile([P, PACK, N], F32, name=f"wraw_{m}{z}", tag=f"wraw_{m}{z}", align_bytes=64)
             rows = weights[m][z * K_PASS:(z + 1) * K_PASS, :]
             nc.sync.dma_start(out=w_raw[m, z][:], in_=rows.rearrange("(p j) c -> p j c", j=PACK))
 
-        load_w("g", 0)
-        load_w("h", 0)
         nc.sync.dma_start(offs_t[:], offs)
+        nc.sync.dma_start(cen_t[:], cen)
         load_x(0, 0, PACK)
         load_x(1, 0, 2)
         load_x(1, 2, 1)
         load_x(1, 3, 1)
-        load_w("g", 1)
-        load_w("h", 1)
-        load_w("s", 0)
-        load_w("s", 1)
-        nc.sync.dma_start(cen_t[:], cen)
+        for m in "gh":
+            for z in range(PASSES):
+                load_w(m, z)
+        s_raw = keep.tile([P, PASSES, PACK, N], F32, name="s_raw", tag="s_raw", align_bytes=64)
+        for z in range(PASSES):
+            rows = w2[z * K_PASS:(z + 1) * K_PASS, :]
+            nc.sync.dma_start(out=s_raw[:, z, :, :], in_=rows.rearrange("(p j) c -> p j c", j=PACK))
         nc.sync.dma_start(pos1_t[:], pos1)
         nc.sync.dma_start(pos2_t[:], pos2)
 
+        w_il = {}
         w_codes = {}
         w_scales = {}
 
-        def rounded_tile(pieces, tag):
-            return keep.tile([P, len(pieces), N, PACK], BF16, name="wil_" + tag, tag=tag, align_bytes=64)
-
-        def round_w(piece, copy, place):
+        def round_w(piece, copy, c0=0, c1=N):
+            if piece not in w_il:
+                w_il[piece] = keep.tile([P, N, PACK], BF16, name=f"wil_{piece[0]}{piece[1]}", align_bytes=64)
             copy(
-                out=place.rearrange("p (c i) j -> p c j i", i=4),
-                in_=w_raw[piece][:].rearrange("p j (c i) -> p c j i", i=4),
+                out=w_il[piece][:, c0:c1, :].rearrange("p (c i) j -> p c j i", i=4),
+                in_=w_raw[piece][:, :, c0:c1].rearrange("p j (c i) -> p c j i", i=4),
             )
 
-        def quant_w(pieces, rounded, tag):
-            if len(pieces) > 1:
-                codes = laid.tile([P, len(pieces) * N], U32, name="wc_" + tag, offset=4 * S, align_bytes=64)
-            else:
-                codes = keep.tile([P, len(pieces) * N], U32, name="wc_" + tag, tag=tag, align_bytes=64)
-            scales = keep.tile([P, len(pieces) * N], U8, name="ws_" + tag, align_bytes=64)
-            nc.vector.quantize_mx(out=codes[:].bitcast(FP8X4), scales=scales[:], in_=rounded[:].rearrange("p a c j -> p (a c j)"))
-            for a, piece in enumerate(pieces):
-                w_codes[piece] = codes[:, a * N:(a + 1) * N]
-                w_scales[piece] = scales[:, a * N:(a + 1) * N]
-
-        def prepare_w(pieces, copy, rounded_tag, codes_tag):
-            rounded = rounded_tile(pieces, rounded_tag)
-            for a, piece in enumerate(pieces):
-                round_w(piece, copy, rounded[:, a, :, :])
-            quant_w(pieces, rounded, codes_tag)
+        def quant_w(piece):
+            w_codes[piece] = keep.tile([P, N], U32, name=f"wc_{piece[0]}{piece[1]}", align_bytes=64)
+            w_scales[piece] = keep.tile([P, N], U8, name=f"ws_{piece[0]}{piece[1]}", align_bytes=64)
+            nc.vector.quantize_mx(
+                out=w_codes[piece][:].bitcast(FP8X4),
+                scales=w_scales[piece][:],
+                in_=w_il[piece][:, :, :].rearrange("p c j -> p (c j)"),
+            )
 
         x_codes = {}
         x_scales = [keep.tile([P, S], U8, name=f"xs{z}", align_bytes=64) for z in range(PASSES)]
         x_il = [keep.tile([P, S, PACK], BF16, name=f"xil{z}", align_bytes=64) for z in range(PASSES)]
 
-        def listed(z, j, c):
-            return plane[z, j].indirect(offs_t[:, c // COLS16:(c + HALF) // COLS16])
+        def listed(z, j, c, n):
+            return plane[z, j].indirect(offs_t[:, c // COLS16:(c + n) // COLS16])
 
-        def gather_planes(z, j0, n):
+        def gather_planes(z, j0, n, on_vector):
             picked = {c: keep.tile([P, n, HALF], F32, name=f"picked{z}{j0}_{c}") for c in (0, HALF)}
-            for c in picked:
-                for i in range(n // 2):
-                    nc.vector.tensor_copy(out=picked[c][:, i, :], in_=listed(z, j0 + i, c))
-                for i in range(n // 2, n):
-                    nc.scalar.activation(out=picked[c][:, i, :], in_=listed(z, j0 + i, c), func=ACT.Copy)
+            for c, nv in zip(picked, on_vector):
+                for i in range(nv):
+                    nc.vector.tensor_copy(out=picked[c][:, i, :], in_=listed(z, j0 + i, c, HALF))
+                for i in range(nv, n):
+                    nc.scalar.activation(out=picked[c][:, i, :], in_=listed(z, j0 + i, c, HALF), func=ACT.Copy)
             for c in picked:
                 nc.vector.tensor_copy(
                     out=x_il[z][:, c:c + HALF, j0:j0 + n].rearrange("p (c i) j -> p c j i", i=4),
@@ -123,13 +110,13 @@ def tile_picked_filmg_relu_e_kernel(tc, xT, w1, w2, w3, offs, cen, pos1, pos2, o
 
         def gather_plane(z, j):
             picked = keep.tile([P, HALF], F32, name=f"picked{z}{j}")
-            nc.vector.tensor_copy(out=x_il[z][:, :HALF, j], in_=listed(z, j, 0))
-            nc.scalar.activation(out=picked[:], in_=listed(z, j, HALF), func=ACT.Copy)
+            nc.vector.tensor_copy(out=x_il[z][:, :HALF, j], in_=listed(z, j, 0, HALF))
+            nc.scalar.activation(out=picked[:], in_=listed(z, j, HALF, HALF), func=ACT.Copy)
             nc.vector.tensor_copy(out=x_il[z][:, HALF:, j], in_=picked[:])
 
         def quant_x(z, c0, codes, width):
             for c in range(0, codes.shape[1], QUARTER):
-                x_codes[z, c0 + c] = codes[:, c:]
+                x_codes[z, c0 + c] = codes[:, c:c + QUARTER]
             for c in range(0, codes.shape[1], width):
                 nc.vector.quantize_mx(
                     out=codes[:, c:c + width].bitcast(FP8X4),
@@ -137,79 +124,95 @@ def tile_picked_filmg_relu_e_kernel(tc, xT, w1, w2, w3, offs, cen, pos1, pos2, o
                     in_=x_il[z][:, c0 + c:c0 + c + width, :].rearrange("p c j -> p (c j)"),
                 )
 
-        cut = {"g": QUARTER, "h": HALF, "s": HALF}
-        banks = {(m, c): psum.tile([P, cut[m]], F32, name=f"bank_{m}{c}") for m in cut for c in range(0, S, cut[m])}
+        quarters = range(0, S, QUARTER)
+        banks = {}
         prod = {}
 
-        def product(m, z, c0, c1):
-            for c in range(c0, c1, cut[m]):
+        def product(m, z):
+            for c in quarters:
+                if z == 0:
+                    banks[m, c] = psum.tile([P, QUARTER], F32, name=f"bank_{m}{c}", tag=f"bank_{'h' if m == 'h' else 'gs'}{c}")
                 nc.tensor.matmul_mx(
                     out=banks[m, c][:],
-                    lhsT=w_codes[m, z].bitcast(FP8X4),
-                    lhsT_scale=w_scales[m, z],
-                    rhs=x_codes[z, c][:, :cut[m]].bitcast(FP8X4),
-                    rhs_scale=x_scales[z][:, c:c + cut[m]],
+                    lhsT=w_codes[m, z][:].bitcast(FP8X4),
+                    lhsT_scale=w_scales[m, z][:],
+                    rhs=x_codes[z, c].bitcast(FP8X4),
+                    rhs_scale=x_scales[z][:, c:c + QUARTER],
                     start=(z == 0),
                     stop=(z == PASSES - 1),
                 )
 
-        def leave_psum(m, tag):
+        def leave_psum(m, tag, on_vector):
             prod[m] = keep.tile([P, S], F32, name=f"{m}_sb", tag=tag, align_bytes=64)
-            for c in range(0, S, cut[m]):
-                nc.scalar.copy(out=prod[m][:, c:c + cut[m]], in_=banks[m, c][:])
+            for c in quarters:
+                copy = nc.vector.tensor_copy if c >= S - on_vector * QUARTER else nc.scalar.copy
+                copy(out=prod[m][:, c:c + QUARTER], in_=banks[m, c][:])
 
-        gather_planes(0, 0, PACK)
-        quant_x(0, 0, keep.tile([P, HALF], U32, name="xc0a", align_bytes=64), HALF)
-        gather_planes(1, 0, 2)
+        gather_planes(0, 0, PACK, (3, 2))
+        quant_x(0, 0, keep.tile([P, S], U32, name="xc0", align_bytes=64), HALF)
+        gather_planes(1, 0, 2, (1, 0))
         gather_plane(1, 2)
-        quant_x(0, HALF, laid.tile([P, HALF], U32, name="xc0b", offset=0, align_bytes=64), HALF)
-        prepare_w([("g", 0), ("h", 0)], nc.scalar.copy, "r_gh0", "c_gh0")
-        product("g", 0, 0, S)
-        product("h", 0, 0, S)
         gather_plane(1, 3)
-        prepare_w([("g", 1)], nc.scalar.copy, "r_g1", "c_g1")
-        quant_x(1, 0, keep.tile([P, HALF], U32, name="xc1a", tag="wraw_g1", align_bytes=64), QUARTER)
-        prepare_w([("h", 1)], nc.scalar.copy, "r_h1", "c_h1")
-        quant_x(1, HALF, laid.tile([P, HALF], U32, name="xc1b", offset=4 * T, align_bytes=64), QUARTER)
-        s_rounded = [rounded_tile([("s", 0)], "r_s0"), laid.tile([P, 1, N, PACK], BF16, name="r_s1", offset=4 * T + 4 * HALF, align_bytes=64)]
-        round_w(("s", 0), nc.scalar.copy, s_rounded[0][:, 0, :, :])
-        round_w(("s", 1), nc.vector.tensor_copy, s_rounded[1][:, 0, :, :])
+        quant_x(1, 0, keep.tile([P, QUARTER], U32, name="xc1a", align_bytes=64), QUARTER)
+        round_w(("g", 0), nc.scalar.copy)
+        quant_w(("g", 0))
+        product("g", 0)
+        round_w(("g", 1), nc.scalar.copy)
+        quant_w(("g", 1))
+        quant_x(1, QUARTER, keep.tile([P, S - QUARTER], U32, name="xc1b", tag="wraw_g0", align_bytes=64), QUARTER)
+        product("g", 1)
+        round_w(("h", 0), nc.scalar.copy)
+        round_w(("h", 1), nc.vector.tensor_copy)
         for z in range(PASSES):
-            quant_w([("s", z)], s_rounded[z], f"c_s{z}")
-        for c in (0, HALF):
-            product("g", 1, c, c + HALF)
-            product("h", 1, c, c + HALF)
+            quant_w(("h", z))
+            product("h", z)
+        leave_psum("g", "g_sb", 0)
+        gc = keep.tile([P, V], F32, name="gc")
+        nc.scalar.activation(out=gc[:], in_=prod["g"][:].indirect(cen_t[:]), func=ACT.Copy)
+        s_il = keep.tile([P, PASSES, N, PACK], BF16, name="s_il", align_bytes=64)
+        most = N - 16
+        nc.vector.tensor_copy(
+            out=s_il[:, 0, :most, :].rearrange("p (c i) j -> p c j i", i=4),
+            in_=s_raw[:, 0, :, :most].rearrange("p j (c i) -> p c j i", i=4),
+        )
+        nc.vector.tensor_copy(
+            out=s_il[:, :, most:, :].rearrange("p z (c i) j -> p z c j i", i=4),
+            in_=s_raw[:, :, :, most:].rearrange("p z j (c i) -> p z c j i", i=4),
+        )
+        nc.vector.tensor_copy(
+            out=s_il[:, 1, :most, :].rearrange("p (c i) j -> p c j i", i=4),
+            in_=s_raw[:, 1, :, :most].rearrange("p j (c i) -> p c j i", i=4),
+        )
         for z in range(PASSES):
-            product("s", z, 0, S)
+            w_il["s", z] = s_il[:, z, :, :]
+        for z in range(PASSES):
+            quant_w(("s", z))
+            product("s", z)
+        leave_psum("h", "s_raw", 2)
+        leave_psum("s", "s_sb", 0)
 
         ends = [slice(0, V // 2), slice(V // 2, V)]
 
         def fetched(m, places, v):
             return prod[m][:].indirect(places[:, v.start // COLS16:v.stop // COLS16])
 
-        leave_psum("g", "wraw_s0")
-        gc = keep.tile([P, V], F32, name="gc", tag="wraw_s1", align_bytes=64)
-        for v in ends:
-            nc.vector.tensor_copy(out=gc[:, v], in_=fetched("g", cen_t, v))
-        leave_psum("h", "r_s0")
         t1 = keep.tile([P, V], F32, name="t1")
         t2 = keep.tile([P, V], F32, name="t2")
+        nc.vector.tensor_tensor(t1[:], prod["h"][:].indirect(pos1_t[:]), gc[:], ALU.mult)
         for v in ends:
-            nc.vector.tensor_tensor(t1[:, v], fetched("h", pos1_t, v), gc[:, v], ALU.mult)
-        nc.vector.tensor_tensor(t2[:], prod["h"][:].indirect(pos2_t[:]), gc[:], ALU.mult)
-        leave_psum("s", "s_sb")
-        sc = keep.tile([P, V], F32, name="sc")
-        nc.scalar.activation(out=sc[:], in_=prod["s"][:].indirect(cen_t[:]), func=ACT.Copy)
+            nc.vector.tensor_tensor(t2[:, v], fetched("h", pos2_t, v), gc[:, v], ALU.mult)
 
-        u1 = keep.tile([P, V], F32, name="u1")
+        a, b = ends
         r1 = keep.tile([P, V], F32, name="r1")
         u2 = keep.tile([P, V], F32, name="u2")
+        sc = keep.tile([P, V // 2], F32, name="sc")
         res = keep.tile([P, V], F32, name="res")
+        nc.scalar.activation(out=sc[:], in_=fetched("s", cen_t, b), func=ACT.Copy)
         for v in ends:
-            nc.vector.tensor_tensor(u1[:, v], t1[:, v], sc[:, v], ALU.add)
-            nc.scalar.activation(out=r1[:, v], in_=u1[:, v], func=ACT.Relu)
-        for v in ends:
-            nc.vector.tensor_tensor(u2[:, v], t2[:, v], sc[:, v], ALU.add)
+            nc.vector.tensor_tensor(gc[:, v], fetched("s", cen_t, v), t1[:, v], ALU.add)
+            nc.scalar.activation(out=r1[:, v], in_=gc[:, v], func=ACT.Relu)
+        nc.vector.tensor_tensor(u2[:, a], fetched("s", cen_t, a), t2[:, a], ALU.add)
+        nc.vector.tensor_tensor(u2[:, b], sc[:], t2[:, b], ALU.add)
         for v in ends:
             nc.vector.scalar_tensor_tensor(out=res[:, v], in0=u2[:, v], scalar=0.0, in1=r1[:, v], op0=ALU.max, op1=ALU.add)
             nc.sync.dma_start(out=out[:, v], in_=res[:, v])

@@ -41,7 +41,10 @@ def tile_picked_filmg_relu_e_kernel(tc, xT, w1, w2, w3, offs, cen, pos1, pos2, o
         w_raw = {}
 
         def load_x(z, j, n):
-            rows = keep.tile([P, n, T], F32, name=f"x{z}{j}")
+            if (z, j) == (1, 2):
+                rows = laid.tile([P, n, T], F32, name="x12", offset=0, align_bytes=64)
+            else:
+                rows = keep.tile([P, n, T], F32, name=f"x{z}{j}")
             nc.sync.dma_start(out=rows[:], in_=x_rows[z, :, j:j + n, :])
             for i in range(n):
                 plane[z, j + i] = rows[:, i, :]
@@ -51,15 +54,16 @@ def tile_picked_filmg_relu_e_kernel(tc, xT, w1, w2, w3, offs, cen, pos1, pos2, o
             rows = weights[m][z * K_PASS:(z + 1) * K_PASS, :]
             nc.sync.dma_start(out=w_raw[m, z][:], in_=rows.rearrange("(p j) c -> p j c", j=PACK))
 
+        load_w("g", 0)
         nc.sync.dma_start(offs_t[:], offs)
-        nc.sync.dma_start(cen_t[:], cen)
         load_x(0, 0, PACK)
         load_x(1, 0, 2)
+        nc.sync.dma_start(cen_t[:], cen)
         load_x(1, 2, 1)
         load_x(1, 3, 1)
-        for m in "gh":
-            for z in range(PASSES):
-                load_w(m, z)
+        load_w("g", 1)
+        for z in range(PASSES):
+            load_w("h", z)
         s_raw = keep.tile([P, PASSES, PACK, N], F32, name="s_raw", tag="s_raw", align_bytes=64)
         for z in range(PASSES):
             rows = w2[z * K_PASS:(z + 1) * K_PASS, :]
@@ -80,7 +84,10 @@ def tile_picked_filmg_relu_e_kernel(tc, xT, w1, w2, w3, offs, cen, pos1, pos2, o
             )
 
         def quant_w(piece):
-            w_codes[piece] = keep.tile([P, N], U32, name=f"wc_{piece[0]}{piece[1]}", align_bytes=64)
+            if piece == ("g", 0):
+                w_codes[piece] = laid.tile([P, N], U32, name="wc_g0", offset=0, align_bytes=64)
+            else:
+                w_codes[piece] = keep.tile([P, N], U32, name=f"wc_{piece[0]}{piece[1]}", align_bytes=64)
             w_scales[piece] = keep.tile([P, N], U8, name=f"ws_{piece[0]}{piece[1]}", align_bytes=64)
             nc.vector.quantize_mx(
                 out=w_codes[piece][:].bitcast(FP8X4),
@@ -114,59 +121,69 @@ def tile_picked_filmg_relu_e_kernel(tc, xT, w1, w2, w3, offs, cen, pos1, pos2, o
             nc.scalar.activation(out=picked[:], in_=listed(z, j, HALF, HALF), func=ACT.Copy)
             nc.vector.tensor_copy(out=x_il[z][:, HALF:, j], in_=picked[:])
 
-        def quant_x(z, c0, codes, width):
-            for c in range(0, codes.shape[1], QUARTER):
-                x_codes[z, c0 + c] = codes[:, c:c + QUARTER]
-            for c in range(0, codes.shape[1], width):
-                nc.vector.quantize_mx(
-                    out=codes[:, c:c + width].bitcast(FP8X4),
-                    scales=x_scales[z][:, c0 + c:c0 + c + width],
-                    in_=x_il[z][:, c0 + c:c0 + c + width, :].rearrange("p c j -> p (c j)"),
-                )
+        def quant_x(z, c, codes):
+            x_codes[z, c] = codes
+            nc.vector.quantize_mx(
+                out=codes.bitcast(FP8X4),
+                scales=x_scales[z][:, c:c + HALF],
+                in_=x_il[z][:, c:c + HALF, :].rearrange("p c j -> p (c j)"),
+            )
 
-        quarters = range(0, S, QUARTER)
+        halves = (0, HALF)
         banks = {}
         prod = {}
 
         def product(m, z):
-            for c in quarters:
+            for c in halves:
                 if z == 0:
-                    banks[m, c] = psum.tile([P, QUARTER], F32, name=f"bank_{m}{c}", tag=f"bank_{'h' if m == 'h' else 'gs'}{c}")
+                    banks[m, c] = psum.tile([P, HALF], F32, name=f"bank_{m}{c}")
                 nc.tensor.matmul_mx(
                     out=banks[m, c][:],
                     lhsT=w_codes[m, z][:].bitcast(FP8X4),
                     lhsT_scale=w_scales[m, z][:],
                     rhs=x_codes[z, c].bitcast(FP8X4),
-                    rhs_scale=x_scales[z][:, c:c + QUARTER],
+                    rhs_scale=x_scales[z][:, c:c + HALF],
                     start=(z == 0),
                     stop=(z == PASSES - 1),
                 )
 
-        def leave_psum(m, tag, on_vector):
+        def leave_psum(m, tag, second_copy):
             prod[m] = keep.tile([P, S], F32, name=f"{m}_sb", tag=tag, align_bytes=64)
-            for c in quarters:
-                copy = nc.vector.tensor_copy if c >= S - on_vector * QUARTER else nc.scalar.copy
-                copy(out=prod[m][:, c:c + QUARTER], in_=banks[m, c][:])
+            nc.scalar.copy(out=prod[m][:, :HALF], in_=banks[m, 0][:])
+            second_copy(out=prod[m][:, HALF:], in_=banks[m, HALF][:])
 
-        gather_planes(0, 0, PACK, (3, 2))
-        quant_x(0, 0, keep.tile([P, S], U32, name="xc0", align_bytes=64), HALF)
-        gather_planes(1, 0, 2, (1, 0))
-        gather_plane(1, 2)
-        gather_plane(1, 3)
-        quant_x(1, 0, keep.tile([P, QUARTER], U32, name="xc1a", align_bytes=64), QUARTER)
         round_w(("g", 0), nc.scalar.copy)
+        gather_planes(0, 0, PACK, (2, 2))
+        first_codes = keep.tile([P, S], U32, name="xc0", align_bytes=64)
+        for c in halves:
+            quant_x(0, c, first_codes[:, c:c + HALF])
+        gather_planes(1, 0, 2, (1, 1))
+        gather_plane(1, 2)
         quant_w(("g", 0))
         product("g", 0)
+        for c in halves:
+            unread = psum.tile([32, S], F32, name=f"unread{c}")
+            nc.tensor.matmul_mx(
+                out=unread[:],
+                lhsT=w_codes["g", 0][:, :32].bitcast(FP8X4),
+                lhsT_scale=w_scales["g", 0][:, :32],
+                rhs=first_codes[:].bitcast(FP8X4),
+                rhs_scale=x_scales[0][:],
+                start=True,
+                stop=True,
+            )
+        gather_plane(1, 3)
+        quant_x(1, 0, keep.tile([P, HALF], U32, name="xc1a", align_bytes=64)[:])
         round_w(("g", 1), nc.scalar.copy)
         quant_w(("g", 1))
-        quant_x(1, QUARTER, keep.tile([P, S - QUARTER], U32, name="xc1b", tag="wraw_g0", align_bytes=64), QUARTER)
+        quant_x(1, HALF, keep.tile([P, HALF], U32, name="xc1b", tag="wraw_g1", align_bytes=64)[:])
         product("g", 1)
         round_w(("h", 0), nc.scalar.copy)
-        round_w(("h", 1), nc.vector.tensor_copy)
+        round_w(("h", 1), nc.scalar.copy)
         for z in range(PASSES):
             quant_w(("h", z))
             product("h", z)
-        leave_psum("g", "g_sb", 0)
+        leave_psum("g", "g_sb", nc.scalar.copy)
         gc = keep.tile([P, V], F32, name="gc")
         nc.scalar.activation(out=gc[:], in_=prod["g"][:].indirect(cen_t[:]), func=ACT.Copy)
         s_il = keep.tile([P, PASSES, N, PACK], BF16, name="s_il", align_bytes=64)
@@ -188,8 +205,8 @@ def tile_picked_filmg_relu_e_kernel(tc, xT, w1, w2, w3, offs, cen, pos1, pos2, o
         for z in range(PASSES):
             quant_w(("s", z))
             product("s", z)
-        leave_psum("h", "s_raw", 2)
-        leave_psum("s", "s_sb", 0)
+        leave_psum("h", "s_raw", nc.vector.tensor_copy)
+        leave_psum("s", "s_sb", nc.scalar.copy)
 
         ends = [slice(0, V // 2), slice(V // 2, V)]
 
@@ -199,20 +216,21 @@ def tile_picked_filmg_relu_e_kernel(tc, xT, w1, w2, w3, offs, cen, pos1, pos2, o
         t1 = keep.tile([P, V], F32, name="t1")
         t2 = keep.tile([P, V], F32, name="t2")
         nc.vector.tensor_tensor(t1[:], prod["h"][:].indirect(pos1_t[:]), gc[:], ALU.mult)
-        for v in ends:
-            nc.vector.tensor_tensor(t2[:, v], fetched("h", pos2_t, v), gc[:, v], ALU.mult)
+        nc.vector.tensor_tensor(t2[:], prod["h"][:].indirect(pos2_t[:]), gc[:], ALU.mult)
 
         a, b = ends
+        u1 = keep.tile([P, V], F32, name="u1")
         r1 = keep.tile([P, V], F32, name="r1")
         u2 = keep.tile([P, V], F32, name="u2")
-        sc = keep.tile([P, V // 2], F32, name="sc")
+        sc = keep.tile([P, V], F32, name="sc")
         res = keep.tile([P, V], F32, name="res")
-        nc.scalar.activation(out=sc[:], in_=fetched("s", cen_t, b), func=ACT.Copy)
+        for v in (b, a):
+            nc.scalar.activation(out=sc[:, v], in_=fetched("s", cen_t, v), func=ACT.Copy)
+        nc.vector.tensor_tensor(u1[:, a], fetched("s", cen_t, a), t1[:, a], ALU.add)
+        nc.vector.tensor_tensor(u1[:, b], sc[:, b], t1[:, b], ALU.add)
+        for v in (b, a):
+            nc.vector.tensor_tensor(u2[:, v], sc[:, v], t2[:, v], ALU.add)
         for v in ends:
-            nc.vector.tensor_tensor(gc[:, v], fetched("s", cen_t, v), t1[:, v], ALU.add)
-            nc.scalar.activation(out=r1[:, v], in_=gc[:, v], func=ACT.Relu)
-        nc.vector.tensor_tensor(u2[:, a], fetched("s", cen_t, a), t2[:, a], ALU.add)
-        nc.vector.tensor_tensor(u2[:, b], sc[:], t2[:, b], ALU.add)
-        for v in ends:
+            nc.scalar.activation(out=r1[:, v], in_=u1[:, v], func=ACT.Relu)
             nc.vector.scalar_tensor_tensor(out=res[:, v], in0=u2[:, v], scalar=0.0, in1=r1[:, v], op0=ALU.max, op1=ALU.add)
             nc.sync.dma_start(out=out[:, v], in_=res[:, v])

@@ -41,8 +41,8 @@ def tile_picked_filmg_relu_e_kernel(tc, xT, w1, w2, w3, offs, cen, pos1, pos2, o
         w_raw = {}
 
         def load_x(z, j, n):
-            if (z, j) == (1, 2):
-                rows = laid.tile([P, n, T], F32, name="x12", offset=0, align_bytes=64)
+            if n == 1:
+                rows = laid.tile([P, n, T], F32, name=f"x{z}{j}", offset=4 * T * (j - 2), align_bytes=64)
             else:
                 rows = keep.tile([P, n, T], F32, name=f"x{z}{j}")
             nc.sync.dma_start(out=rows[:], in_=x_rows[z, :, j:j + n, :])
@@ -173,7 +173,7 @@ def tile_picked_filmg_relu_e_kernel(tc, xT, w1, w2, w3, offs, cen, pos1, pos2, o
                 stop=True,
             )
         gather_plane(1, 3)
-        quant_x(1, 0, keep.tile([P, HALF], U32, name="xc1a", align_bytes=64)[:])
+        quant_x(1, 0, laid.tile([P, HALF], U32, name="xc1a", offset=4 * T, align_bytes=64)[:])
         round_w(("g", 1), nc.scalar.copy)
         quant_w(("g", 1))
         quant_x(1, HALF, keep.tile([P, HALF], U32, name="xc1b", tag="wraw_g1", align_bytes=64)[:])
@@ -187,7 +187,7 @@ def tile_picked_filmg_relu_e_kernel(tc, xT, w1, w2, w3, offs, cen, pos1, pos2, o
         gc = keep.tile([P, V], F32, name="gc")
         nc.scalar.activation(out=gc[:], in_=prod["g"][:].indirect(cen_t[:]), func=ACT.Copy)
         s_il = keep.tile([P, PASSES, N, PACK], BF16, name="s_il", align_bytes=64)
-        most = N - 16
+        most = N - 8
         nc.vector.tensor_copy(
             out=s_il[:, 0, :most, :].rearrange("p (c i) j -> p c j i", i=4),
             in_=s_raw[:, 0, :, :most].rearrange("p j (c i) -> p c j i", i=4),
@@ -228,8 +228,7 @@ def tile_picked_filmg_relu_e_kernel(tc, xT, w1, w2, w3, offs, cen, pos1, pos2, o
             nc.scalar.activation(out=sc[:, v], in_=fetched("s", cen_t, v), func=ACT.Copy)
         nc.vector.tensor_tensor(u1[:, a], fetched("s", cen_t, a), t1[:, a], ALU.add)
         nc.vector.tensor_tensor(u1[:, b], sc[:, b], t1[:, b], ALU.add)
-        for v in (b, a):
-            nc.vector.tensor_tensor(u2[:, v], sc[:, v], t2[:, v], ALU.add)
+        nc.vector.tensor_tensor(u2[:], sc[:], t2[:], ALU.add)
         for v in ends:
             nc.scalar.activation(out=r1[:, v], in_=u1[:, v], func=ACT.Relu)
             nc.vector.scalar_tensor_tensor(out=res[:, v], in0=u2[:, v], scalar=0.0, in1=r1[:, v], op0=ALU.max, op1=ALU.add)

@@ -58,14 +58,15 @@ def tile_picked_filmg_relu_e_kernel(tc, xT, w1, w2, w3, offs, cen, pos1, pos2, o
         nc.sync.dma_start(offs_t[:], offs)
         load_x(0, 0, PACK)
         load_x(1, 0, 2)
-        nc.sync.dma_start(cen_t[:], cen)
         load_x(1, 2, 1)
         load_x(1, 3, 1)
         load_w("g", 1)
         for z in range(PASSES):
             load_w("h", z)
-        s_raw = keep.tile([P, PASSES, PACK, N], F32, name="s_raw", tag="s_raw", align_bytes=64)
+        s_raw = laid.tile([P, PASSES, PACK, N], F32, name="s_raw", offset=8 * T, align_bytes=64)
         for z in range(PASSES):
+            if z == 1:
+                nc.sync.dma_start(cen_t[:], cen)
             rows = w2[z * K_PASS:(z + 1) * K_PASS, :]
             nc.sync.dma_start(out=s_raw[:, z, :, :], in_=rows.rearrange("(p j) c -> p j c", j=PACK))
         nc.sync.dma_start(pos1_t[:], pos1)
@@ -147,8 +148,11 @@ def tile_picked_filmg_relu_e_kernel(tc, xT, w1, w2, w3, offs, cen, pos1, pos2, o
                     stop=(z == PASSES - 1),
                 )
 
-        def leave_psum(m, tag, second_copy):
-            prod[m] = keep.tile([P, S], F32, name=f"{m}_sb", tag=tag, align_bytes=64)
+        def leave_psum(m, second_copy):
+            if m == "h":
+                prod[m] = laid.tile([P, S], F32, name="h_sb", offset=8 * T, align_bytes=64)
+            else:
+                prod[m] = keep.tile([P, S], F32, name=f"{m}_sb", align_bytes=64)
             nc.scalar.copy(out=prod[m][:, :HALF], in_=banks[m, 0][:])
             second_copy(out=prod[m][:, HALF:], in_=banks[m, HALF][:])
 
@@ -183,9 +187,15 @@ def tile_picked_filmg_relu_e_kernel(tc, xT, w1, w2, w3, offs, cen, pos1, pos2, o
         for z in range(PASSES):
             quant_w(("h", z))
             product("h", z)
-        leave_psum("g", "g_sb", nc.scalar.copy)
-        gc = keep.tile([P, V], F32, name="gc")
-        nc.scalar.activation(out=gc[:], in_=prod["g"][:].indirect(cen_t[:]), func=ACT.Copy)
+        ends = [slice(0, V // 2), slice(V // 2, V)]
+        a, b = ends
+
+        def fetched(m, places, v):
+            return prod[m][:].indirect(places[:, v.start // COLS16:v.stop // COLS16])
+
+        leave_psum("g", nc.scalar.copy)
+        gc_a = keep.tile([P, V // 2], F32, name="gc_a")
+        nc.scalar.activation(out=gc_a[:], in_=fetched("g", cen_t, a), func=ACT.Copy)
         s_il = keep.tile([P, PASSES, N, PACK], BF16, name="s_il", align_bytes=64)
         most = N - 8
         nc.vector.tensor_copy(
@@ -205,20 +215,17 @@ def tile_picked_filmg_relu_e_kernel(tc, xT, w1, w2, w3, offs, cen, pos1, pos2, o
         for z in range(PASSES):
             quant_w(("s", z))
             product("s", z)
-        leave_psum("h", "s_raw", nc.vector.tensor_copy)
-        leave_psum("s", "s_sb", nc.scalar.copy)
-
-        ends = [slice(0, V // 2), slice(V // 2, V)]
-
-        def fetched(m, places, v):
-            return prod[m][:].indirect(places[:, v.start // COLS16:v.stop // COLS16])
+        leave_psum("h", nc.vector.tensor_copy)
+        gc_b = laid.tile([P, V // 2], F32, name="gc_b", offset=8 * T + 4 * S, align_bytes=64)
+        nc.scalar.activation(out=gc_b[:], in_=fetched("g", cen_t, b), func=ACT.Copy)
+        leave_psum("s", nc.scalar.copy)
 
         t1 = keep.tile([P, V], F32, name="t1")
         t2 = keep.tile([P, V], F32, name="t2")
-        nc.vector.tensor_tensor(t1[:], prod["h"][:].indirect(pos1_t[:]), gc[:], ALU.mult)
-        nc.vector.tensor_tensor(t2[:], prod["h"][:].indirect(pos2_t[:]), gc[:], ALU.mult)
+        for t, places in ((t1, pos1_t), (t2, pos2_t)):
+            for v, gc in ((a, gc_a), (b, gc_b)):
+                nc.vector.tensor_tensor(t[:, v], fetched("h", places, v), gc[:], ALU.mult)
 
-        a, b = ends
         u1 = keep.tile([P, V], F32, name="u1")
         r1 = keep.tile([P, V], F32, name="r1")
         u2 = keep.tile([P, V], F32, name="u2")
@@ -228,7 +235,8 @@ def tile_picked_filmg_relu_e_kernel(tc, xT, w1, w2, w3, offs, cen, pos1, pos2, o
             nc.scalar.activation(out=sc[:, v], in_=fetched("s", cen_t, v), func=ACT.Copy)
         nc.vector.tensor_tensor(u1[:, a], fetched("s", cen_t, a), t1[:, a], ALU.add)
         nc.vector.tensor_tensor(u1[:, b], sc[:, b], t1[:, b], ALU.add)
-        nc.vector.tensor_tensor(u2[:], sc[:], t2[:], ALU.add)
+        for v in (b, a):
+            nc.vector.tensor_tensor(u2[:, v], sc[:, v], t2[:, v], ALU.add)
         for v in ends:
             nc.scalar.activation(out=r1[:, v], in_=u1[:, v], func=ACT.Relu)
             nc.vector.scalar_tensor_tensor(out=res[:, v], in0=u2[:, v], scalar=0.0, in1=r1[:, v], op0=ALU.max, op1=ALU.add)

@@ -58,6 +58,7 @@ def tile_picked_filmg_relu_e_kernel(tc, xT, w1, w2, w3, offs, cen, pos1, pos2, o
         nc.sync.dma_start(offs_t[:], offs)
         load_x(0, 0, PACK)
         load_x(1, 0, 2)
+        nc.sync.dma_start(cen_t[:], cen)
         load_x(1, 2, 1)
         load_x(1, 3, 1)
         load_w("g", 1)
@@ -65,8 +66,6 @@ def tile_picked_filmg_relu_e_kernel(tc, xT, w1, w2, w3, offs, cen, pos1, pos2, o
             load_w("h", z)
         s_raw = laid.tile([P, PASSES, PACK, N], F32, name="s_raw", offset=8 * T, align_bytes=64)
         for z in range(PASSES):
-            if z == 1:
-                nc.sync.dma_start(cen_t[:], cen)
             rows = w2[z * K_PASS:(z + 1) * K_PASS, :]
             nc.sync.dma_start(out=s_raw[:, z, :, :], in_=rows.rearrange("(p j) c -> p j c", j=PACK))
         nc.sync.dma_start(pos1_t[:], pos1)
@@ -183,7 +182,8 @@ def tile_picked_filmg_relu_e_kernel(tc, xT, w1, w2, w3, offs, cen, pos1, pos2, o
         quant_x(1, HALF, keep.tile([P, HALF], U32, name="xc1b", tag="wraw_g1", align_bytes=64)[:])
         product("g", 1)
         round_w(("h", 0), nc.scalar.copy)
-        round_w(("h", 1), nc.scalar.copy)
+        round_w(("h", 1), nc.vector.tensor_copy, 0, 16)
+        round_w(("h", 1), nc.scalar.copy, 16, N)
         for z in range(PASSES):
             quant_w(("h", z))
             product("h", z)

@@ -19,8 +19,8 @@ PACK = 4
 K_PASS = P * PACK
 PASSES = K // K_PASS
 HALF = S // 2
-QUARTER = S // 4
 COLS16 = 16
+PLANE_BYTES = 4 * T
 
 
 def tile_picked_filmg_relu_e_kernel(tc, xT, w1, w2, w3, offs, cen, pos1, pos2, out):
@@ -36,48 +36,50 @@ def tile_picked_filmg_relu_e_kernel(tc, xT, w1, w2, w3, offs, cen, pos1, pos2, o
         pos2_t = keep.tile([P, V // COLS16], U16, name="pos2_t")
 
         x_rows = xT.rearrange("(z p j) t -> z p j t", z=PASSES, j=PACK)
-        weights = {"g": w1, "s": w2, "h": w3}
         plane = {}
-        w_raw = {}
 
         def load_x(z, j, n):
             if n == 1:
-                rows = laid.tile([P, n, T], F32, name=f"x{z}{j}", offset=4 * T * (j - 2), align_bytes=64)
+                rows = laid.tile([P, n, T], F32, name=f"x{z}{j}", offset=PLANE_BYTES * (j - 2), align_bytes=64)
             else:
                 rows = keep.tile([P, n, T], F32, name=f"x{z}{j}")
             nc.sync.dma_start(out=rows[:], in_=x_rows[z, :, j:j + n, :])
             for i in range(n):
                 plane[z, j + i] = rows[:, i, :]
 
-        def load_w(m, z):
-            w_raw[m, z] = keep.tile([P, PACK, N], F32, name=f"wraw_{m}{z}", tag=f"wraw_{m}{z}", align_bytes=64)
-            rows = weights[m][z * K_PASS:(z + 1) * K_PASS, :]
-            nc.sync.dma_start(out=w_raw[m, z][:], in_=rows.rearrange("(p j) c -> p j c", j=PACK))
+        def by_pass(w):
+            return w.rearrange("(z p j) c -> p z j c", z=PASSES, j=PACK)
 
-        load_w("g", 0)
+        g_raw = [keep.tile([P, PACK, N], F32, name=f"g_raw{z}", tag=f"g_raw{z}", align_bytes=64) for z in range(PASSES)]
+        nc.sync.dma_start(out=g_raw[0][:], in_=by_pass(w1)[:, 0])
         nc.sync.dma_start(offs_t[:], offs)
         load_x(0, 0, PACK)
         load_x(1, 0, 2)
-        nc.sync.dma_start(cen_t[:], cen)
         load_x(1, 2, 1)
         load_x(1, 3, 1)
-        load_w("g", 1)
+        nc.sync.dma_start(out=g_raw[1][:], in_=by_pass(w1)[:, 1])
+        h_raw = [keep.tile([P, PACK, N], F32, name=f"h_raw{z}", tag=f"h_raw{z}", align_bytes=64) for z in range(PASSES)]
         for z in range(PASSES):
-            load_w("h", z)
-        s_raw = laid.tile([P, PASSES, PACK, N], F32, name="s_raw", offset=8 * T, align_bytes=64)
+            nc.sync.dma_start(out=h_raw[z][:], in_=by_pass(w3)[:, z])
+        s_raw = keep.tile([P, PASSES, PACK, N], F32, name="s_raw", align_bytes=64)
         for z in range(PASSES):
-            rows = w2[z * K_PASS:(z + 1) * K_PASS, :]
-            nc.sync.dma_start(out=s_raw[:, z, :, :], in_=rows.rearrange("(p j) c -> p j c", j=PACK))
+            nc.sync.dma_start(out=s_raw[:, z], in_=by_pass(w2)[:, z])
+        nc.sync.dma_start(cen_t[:], cen)
         nc.sync.dma_start(pos1_t[:], pos1)
         nc.sync.dma_start(pos2_t[:], pos2)
 
-        w_il = {}
+        w_raw = {("g", z): g_raw[z][:] for z in range(PASSES)}
+        w_raw.update({("h", z): h_raw[z][:] for z in range(PASSES)})
+        w_raw.update({("s", z): s_raw[:, z] for z in range(PASSES)})
+        s_il = keep.tile([P, PASSES, N, PACK], BF16, name="s_il", align_bytes=64)
+        w_il = {("s", z): s_il[:, z] for z in range(PASSES)}
+        for m in "gh":
+            for z in range(PASSES):
+                w_il[m, z] = keep.tile([P, N, PACK], BF16, name=f"wil_{m}{z}", align_bytes=64)[:]
         w_codes = {}
         w_scales = {}
 
         def round_w(piece, copy, c0=0, c1=N):
-            if piece not in w_il:
-                w_il[piece] = keep.tile([P, N, PACK], BF16, name=f"wil_{piece[0]}{piece[1]}", align_bytes=64)
             copy(
                 out=w_il[piece][:, c0:c1, :].rearrange("p (c i) j -> p c j i", i=4),
                 in_=w_raw[piece][:, :, c0:c1].rearrange("p j (c i) -> p c j i", i=4),
@@ -92,7 +94,7 @@ def tile_picked_filmg_relu_e_kernel(tc, xT, w1, w2, w3, offs, cen, pos1, pos2, o
             nc.vector.quantize_mx(
                 out=w_codes[piece][:].bitcast(FP8X4),
                 scales=w_scales[piece][:],
-                in_=w_il[piece][:, :, :].rearrange("p c j -> p (c j)"),
+                in_=w_il[piece].rearrange("p c j -> p (c j)"),
             )
 
         x_codes = {}
@@ -147,13 +149,10 @@ def tile_picked_filmg_relu_e_kernel(tc, xT, w1, w2, w3, offs, cen, pos1, pos2, o
                     stop=(z == PASSES - 1),
                 )
 
-        def leave_psum(m, second_copy):
-            if m == "h":
-                prod[m] = laid.tile([P, S], F32, name="h_sb", offset=8 * T, align_bytes=64)
-            else:
-                prod[m] = keep.tile([P, S], F32, name=f"{m}_sb", align_bytes=64)
-            nc.scalar.copy(out=prod[m][:, :HALF], in_=banks[m, 0][:])
-            second_copy(out=prod[m][:, HALF:], in_=banks[m, HALF][:])
+        def leave_psum(m, tag):
+            prod[m] = keep.tile([P, S], F32, name=f"{m}_sb", tag=tag, align_bytes=64)
+            for c in halves:
+                nc.scalar.copy(out=prod[m][:, c:c + HALF], in_=banks[m, c][:])
 
         round_w(("g", 0), nc.scalar.copy)
         gather_planes(0, 0, PACK, (2, 2))
@@ -176,68 +175,61 @@ def tile_picked_filmg_relu_e_kernel(tc, xT, w1, w2, w3, offs, cen, pos1, pos2, o
                 stop=True,
             )
         gather_plane(1, 3)
-        quant_x(1, 0, laid.tile([P, HALF], U32, name="xc1a", offset=4 * T, align_bytes=64)[:])
+        quant_x(1, 0, laid.tile([P, HALF], U32, name="xc1a", offset=PLANE_BYTES, align_bytes=64)[:])
         round_w(("g", 1), nc.scalar.copy)
         quant_w(("g", 1))
-        quant_x(1, HALF, keep.tile([P, HALF], U32, name="xc1b", tag="wraw_g1", align_bytes=64)[:])
+        quant_x(1, HALF, keep.tile([P, HALF], U32, name="xc1b", tag="g_raw1", align_bytes=64)[:])
         product("g", 1)
         round_w(("h", 0), nc.scalar.copy)
-        round_w(("h", 1), nc.vector.tensor_copy, 0, 16)
-        round_w(("h", 1), nc.scalar.copy, 16, N)
+        round_w(("h", 1), nc.vector.tensor_copy, 0, 48)
+        round_w(("h", 1), nc.scalar.copy, 48, N)
         for z in range(PASSES):
             quant_w(("h", z))
             product("h", z)
+        leave_psum("g", "g_sb")
+        most = N - 8
+        round_w(("s", 0), nc.vector.tensor_copy, 0, most)
+        nc.vector.tensor_copy(
+            out=s_il[:, :, most:, :].rearrange("p z (c i) j -> p z c j i", i=4),
+            in_=s_raw[:, :, :, most:].rearrange("p z j (c i) -> p z c j i", i=4),
+        )
+        round_w(("s", 1), nc.vector.tensor_copy, 0, most)
+        for z in range(PASSES):
+            quant_w(("s", z))
+            product("s", z)
+        leave_psum("h", "h_sb")
         ends = [slice(0, V // 2), slice(V // 2, V)]
         a, b = ends
 
         def fetched(m, places, v):
             return prod[m][:].indirect(places[:, v.start // COLS16:v.stop // COLS16])
 
-        leave_psum("g", nc.scalar.copy)
-        gc_a = keep.tile([P, V // 2], F32, name="gc_a")
-        nc.scalar.activation(out=gc_a[:], in_=fetched("g", cen_t, a), func=ACT.Copy)
-        s_il = keep.tile([P, PASSES, N, PACK], BF16, name="s_il", align_bytes=64)
-        most = N - 8
-        nc.vector.tensor_copy(
-            out=s_il[:, 0, :most, :].rearrange("p (c i) j -> p c j i", i=4),
-            in_=s_raw[:, 0, :, :most].rearrange("p j (c i) -> p c j i", i=4),
-        )
-        nc.vector.tensor_copy(
-            out=s_il[:, :, most:, :].rearrange("p z (c i) j -> p z c j i", i=4),
-            in_=s_raw[:, :, :, most:].rearrange("p z j (c i) -> p z c j i", i=4),
-        )
-        nc.vector.tensor_copy(
-            out=s_il[:, 1, :most, :].rearrange("p (c i) j -> p c j i", i=4),
-            in_=s_raw[:, 1, :, :most].rearrange("p j (c i) -> p c j i", i=4),
-        )
-        for z in range(PASSES):
-            w_il["s", z] = s_il[:, z, :, :]
-        for z in range(PASSES):
-            quant_w(("s", z))
-            product("s", z)
-        leave_psum("h", nc.vector.tensor_copy)
-        gc_b = laid.tile([P, V // 2], F32, name="gc_b", offset=8 * T + 4 * S, align_bytes=64)
-        nc.scalar.activation(out=gc_b[:], in_=fetched("g", cen_t, b), func=ACT.Copy)
-        leave_psum("s", nc.scalar.copy)
+        few, many = slice(0, V // 4), slice(V // 4, V)
+        gc_a = keep.tile([P, V // 4], F32, name="gc_a", tag="gc_a")
+        gc_b = keep.tile([P, V - V // 4], F32, name="gc_b")
+        nc.vector.tensor_copy(out=gc_a[:], in_=fetched("g", cen_t, few))
+        nc.scalar.activation(out=gc_b[:], in_=fetched("g", cen_t, many), func=ACT.Copy)
+        leave_psum("s", "s_sb")
 
         t1 = keep.tile([P, V], F32, name="t1")
         t2 = keep.tile([P, V], F32, name="t2")
-        for t, places in ((t1, pos1_t), (t2, pos2_t)):
-            for v, gc in ((a, gc_a), (b, gc_b)):
+        for v, gc in ((few, gc_a), (many, gc_b)):
+            for t, places in ((t1, pos1_t), (t2, pos2_t)):
                 nc.vector.tensor_tensor(t[:, v], fetched("h", places, v), gc[:], ALU.mult)
 
-        u1 = keep.tile([P, V], F32, name="u1")
+        u1_a = keep.tile([P, V // 2], F32, name="u1_a", tag="gc_a")
+        u1_b = keep.tile([P, V // 2], F32, name="u1_b")
         r1 = keep.tile([P, V], F32, name="r1")
         u2 = keep.tile([P, V], F32, name="u2")
         sc = keep.tile([P, V], F32, name="sc")
         res = keep.tile([P, V], F32, name="res")
         for v in (b, a):
             nc.scalar.activation(out=sc[:, v], in_=fetched("s", cen_t, v), func=ACT.Copy)
-        nc.vector.tensor_tensor(u1[:, a], fetched("s", cen_t, a), t1[:, a], ALU.add)
-        nc.vector.tensor_tensor(u1[:, b], sc[:, b], t1[:, b], ALU.add)
+        nc.vector.tensor_tensor(u1_a[:], fetched("s", cen_t, a), t1[:, a], ALU.add)
+        nc.vector.tensor_tensor(u1_b[:], sc[:, b], t1[:, b], ALU.add)
         for v in (b, a):
             nc.vector.tensor_tensor(u2[:, v], sc[:, v], t2[:, v], ALU.add)
-        for v in ends:
-            nc.scalar.activation(out=r1[:, v], in_=u1[:, v], func=ACT.Relu)
+        for v, u1 in ((a, u1_a), (b, u1_b)):
+            nc.scalar.activation(out=r1[:, v], in_=u1[:], func=ACT.Relu)
             nc.vector.scalar_tensor_tensor(out=res[:, v], in0=u2[:, v], scalar=0.0, in1=r1[:, v], op0=ALU.max, op1=ALU.add)
             nc.sync.dma_start(out=out[:, v], in_=res[:, v])

@@ -40,9 +40,9 @@ def tile_picked_filmg_relu_e_kernel(tc, xT, w1, w2, w3, offs, cen, pos1, pos2, o
 
         def load_x(z, j, n):
             if n == 1:
-                rows = laid.tile([P, n, T], F32, name=f"x{z}{j}", offset=PLANE_BYTES * (j - 2), align_bytes=64)
+                rows = laid.tile([P, n, T], F32, name=f"x{z}{j}", offset=PLANE_BYTES * (j - 2), align_bytes=256)
             else:
-                rows = keep.tile([P, n, T], F32, name=f"x{z}{j}")
+                rows = keep.tile([P, n, T], F32, name=f"x{z}{j}", align_bytes=256)
             nc.sync.dma_start(out=rows[:], in_=x_rows[z, :, j:j + n, :])
             for i in range(n):
                 plane[z, j + i] = rows[:, i, :]
@@ -50,7 +50,7 @@ def tile_picked_filmg_relu_e_kernel(tc, xT, w1, w2, w3, offs, cen, pos1, pos2, o
         def by_pass(w):
             return w.rearrange("(z p j) c -> p z j c", z=PASSES, j=PACK)
 
-        g_raw = [keep.tile([P, PACK, N], F32, name=f"g_raw{z}", tag=f"g_raw{z}", align_bytes=64) for z in range(PASSES)]
+        g_raw = [keep.tile([P, PACK, N], F32, name=f"g_raw{z}", tag=f"g_raw{z}", align_bytes=256) for z in range(PASSES)]
         nc.sync.dma_start(out=g_raw[0][:], in_=by_pass(w1)[:, 0])
         nc.sync.dma_start(offs_t[:], offs)
         load_x(0, 0, PACK)
@@ -58,10 +58,10 @@ def tile_picked_filmg_relu_e_kernel(tc, xT, w1, w2, w3, offs, cen, pos1, pos2, o
         load_x(1, 2, 1)
         load_x(1, 3, 1)
         nc.sync.dma_start(out=g_raw[1][:], in_=by_pass(w1)[:, 1])
-        h_raw = [keep.tile([P, PACK, N], F32, name=f"h_raw{z}", tag=f"h_raw{z}", align_bytes=64) for z in range(PASSES)]
+        h_raw = [keep.tile([P, PACK, N], F32, name=f"h_raw{z}", tag=f"h_raw{z}", align_bytes=256) for z in range(PASSES)]
         for z in range(PASSES):
             nc.sync.dma_start(out=h_raw[z][:], in_=by_pass(w3)[:, z])
-        s_raw = keep.tile([P, PASSES, PACK, N], F32, name="s_raw", align_bytes=64)
+        s_raw = keep.tile([P, PASSES, PACK, N], F32, name="s_raw", align_bytes=256)
         for z in range(PASSES):
             nc.sync.dma_start(out=s_raw[:, z], in_=by_pass(w2)[:, z])
         nc.sync.dma_start(cen_t[:], cen)
@@ -178,7 +178,7 @@ def tile_picked_filmg_relu_e_kernel(tc, xT, w1, w2, w3, offs, cen, pos1, pos2, o
         quant_x(1, 0, laid.tile([P, HALF], U32, name="xc1a", offset=PLANE_BYTES, align_bytes=64)[:])
         round_w(("g", 1), nc.scalar.copy)
         quant_w(("g", 1))
-        quant_x(1, HALF, keep.tile([P, HALF], U32, name="xc1b", tag="g_raw1", align_bytes=64)[:])
+        quant_x(1, HALF, keep.tile([P, HALF], U32, name="xc1b", tag="g_raw1", align_bytes=256)[:])
         product("g", 1)
         round_w(("h", 0), nc.scalar.copy)
         round_w(("h", 1), nc.vector.tensor_copy, 0, 48)
@@ -222,7 +222,7 @@ def tile_picked_filmg_relu_e_kernel(tc, xT, w1, w2, w3, offs, cen, pos1, pos2, o
         r1 = keep.tile([P, V], F32, name="r1")
         u2 = keep.tile([P, V], F32, name="u2")
         sc = keep.tile([P, V], F32, name="sc")
-        res = keep.tile([P, V], F32, name="res")
+        res = keep.tile([P, V], F32, name="res", align_bytes=256)
         for v in (b, a):
             nc.scalar.activation(out=sc[:, v], in_=fetched("s", cen_t, v), func=ACT.Copy)
         nc.vector.tensor_tensor(u1_a[:], fetched("s", cen_t, a), t1[:, a], ALU.add)

@@ -188,7 +188,8 @@ def tile_picked_filmg_relu_e_kernel(tc, xT, w1, w2, w3, offs, cen, pos1, pos2, o
             product("h", z)
         leave_psum("g", "g_sb")
         most = N - 8
-        round_w(("s", 0), nc.vector.tensor_copy, 0, most)
+        round_w(("s", 0), nc.scalar.copy, 88, most)
+        round_w(("s", 0), nc.vector.tensor_copy, 0, 88)
         nc.vector.tensor_copy(
             out=s_il[:, :, most:, :].rearrange("p z (c i) j -> p z c j i", i=4),
             in_=s_raw[:, :, :, most:].rearrange("p z j (c i) -> p z c j i", i=4),
@@ -204,9 +205,10 @@ def tile_picked_filmg_relu_e_kernel(tc, xT, w1, w2, w3, offs, cen, pos1, pos2, o
         def fetched(m, places, v):
             return prod[m][:].indirect(places[:, v.start // COLS16:v.stop // COLS16])
 
-        few, many = slice(0, V // 4), slice(V // 4, V)
-        gc_a = keep.tile([P, V // 4], F32, name="gc_a", tag="gc_a")
-        gc_b = keep.tile([P, V - V // 4], F32, name="gc_b")
+        cut = 96
+        few, many = slice(0, cut), slice(cut, V)
+        gc_a = keep.tile([P, cut], F32, name="gc_a", tag="gc_a")
+        gc_b = keep.tile([P, V - cut], F32, name="gc_b")
         nc.vector.tensor_copy(out=gc_a[:], in_=fetched("g", cen_t, few))
         nc.scalar.activation(out=gc_b[:], in_=fetched("g", cen_t, many), func=ACT.Copy)
         leave_psum("s", "s_sb")
@@ -227,7 +229,7 @@ def tile_picked_filmg_relu_e_kernel(tc, xT, w1, w2, w3, offs, cen, pos1, pos2, o
             nc.scalar.activation(out=sc[:, v], in_=fetched("s", cen_t, v), func=ACT.Copy)
         nc.vector.tensor_tensor(u1_a[:], fetched("s", cen_t, a), t1[:, a], ALU.add)
         nc.vector.tensor_tensor(u1_b[:], sc[:, b], t1[:, b], ALU.add)
-        for v in (b, a):
+        for v in (a, b):
             nc.vector.tensor_tensor(u2[:, v], sc[:, v], t2[:, v], ALU.add)
         for v, u1 in ((a, u1_a), (b, u1_b)):
             nc.scalar.activation(out=r1[:, v], in_=u1[:], func=ACT.Relu)

@@ -87,7 +87,7 @@ def tile_picked_filmg_relu_e_kernel(tc, xT, w1, w2, w3, offs, cen, pos1, pos2, o
 
         def quant_w(piece):
             if piece == ("g", 0):
-                w_codes[piece] = laid.tile([P, N], U32, name="wc_g0", offset=0, align_bytes=64)
+                w_codes[piece] = keep.tile([P, N], U32, name="wc_g0", tag="picked12", align_bytes=64)
             else:
                 w_codes[piece] = keep.tile([P, N], U32, name=f"wc_{piece[0]}{piece[1]}", align_bytes=64)
             w_scales[piece] = keep.tile([P, N], U8, name=f"ws_{piece[0]}{piece[1]}", align_bytes=64)
@@ -118,7 +118,7 @@ def tile_picked_filmg_relu_e_kernel(tc, xT, w1, w2, w3, offs, cen, pos1, pos2, o
                 )
 
         def gather_plane(z, j):
-            picked = keep.tile([P, HALF], F32, name=f"picked{z}{j}")
+            picked = keep.tile([P, HALF], F32, name=f"picked{z}{j}", tag=f"picked{z}{j}", align_bytes=64)
             nc.vector.tensor_copy(out=x_il[z][:, :HALF, j], in_=listed(z, j, 0, HALF))
             nc.scalar.activation(out=picked[:], in_=listed(z, j, HALF, HALF), func=ACT.Copy)
             nc.vector.tensor_copy(out=x_il[z][:, HALF:, j], in_=picked[:])
@@ -188,8 +188,8 @@ def tile_picked_filmg_relu_e_kernel(tc, xT, w1, w2, w3, offs, cen, pos1, pos2, o
             product("h", z)
         leave_psum("g", "g_sb")
         most = N - 8
-        round_w(("s", 0), nc.scalar.copy, 88, most)
-        round_w(("s", 0), nc.vector.tensor_copy, 0, 88)
+        round_w(("s", 0), nc.scalar.copy, 104, most)
+        round_w(("s", 0), nc.vector.tensor_copy, 0, 104)
         nc.vector.tensor_copy(
             out=s_il[:, :, most:, :].rearrange("p z (c i) j -> p z c j i", i=4),
             in_=s_raw[:, :, :, most:].rearrange("p z j (c i) -> p z c j i", i=4),

@@ -188,8 +188,7 @@ def tile_picked_filmg_relu_e_kernel(tc, xT, w1, w2, w3, offs, cen, pos1, pos2, o
             product("h", z)
         leave_psum("g", "g_sb")
         most = N - 8
-        round_w(("s", 0), nc.scalar.copy, 104, most)
-        round_w(("s", 0), nc.vector.tensor_copy, 0, 104)
+        round_w(("s", 0), nc.vector.tensor_copy, 0, most)
         nc.vector.tensor_copy(
             out=s_il[:, :, most:, :].rearrange("p z (c i) j -> p z c j i", i=4),
             in_=s_raw[:, :, :, most:].rearrange("p z j (c i) -> p z c j i", i=4),
@@ -205,7 +204,7 @@ def tile_picked_filmg_relu_e_kernel(tc, xT, w1, w2, w3, offs, cen, pos1, pos2, o
         def fetched(m, places, v):
             return prod[m][:].indirect(places[:, v.start // COLS16:v.stop // COLS16])
 
-        cut = 96
+        cut = V // 4
         few, many = slice(0, cut), slice(cut, V)
         gc_a = keep.tile([P, cut], F32, name="gc_a", tag="gc_a")
         gc_b = keep.tile([P, V - cut], F32, name="gc_b")

from contextlib import ExitStack

import concourse.mybir as mybir

K, T, S, V, N = 1024, 2048, 512, 256, 128
FLOPS = 3 * 2 * K * S * N

F32 = mybir.dt.float32
BF16 = mybir.dt.bfloat16
U32 = mybir.dt.uint32
U16 = mybir.dt.uint16
U8 = mybir.dt.uint8
FP8X4 = mybir.dt.float8_e4m3fn_x4
ALU = mybir.AluOpType
ACT = mybir.ActivationFunctionType

P = 128
PACK = 4
K_PASS = P * PACK
PASSES = K // K_PASS
HALF = S // 2
COLS16 = 16
PLANE_BYTES = 4 * T


def tile_picked_filmg_relu_e_kernel(tc, xT, w1, w2, w3, offs, cen, pos1, pos2, out):
    nc = tc.nc
    with ExitStack() as ctx:
        keep = ctx.enter_context(tc.tile_pool(name="keep", bufs=1))
        laid = ctx.enter_context(tc.tile_pool(name="laid", bufs=1))
        psum = ctx.enter_context(tc.psum_pool(name="psum", bufs=1))

        offs_t = keep.tile([P, S // COLS16], U16, name="offs_t")
        cen_t = keep.tile([P, V // COLS16], U16, name="cen_t")
        pos1_t = keep.tile([P, V // COLS16], U16, name="pos1_t")
        pos2_t = keep.tile([P, V // COLS16], U16, name="pos2_t")

        x_rows = xT.rearrange("(z p j) t -> z p j t", z=PASSES, j=PACK)
        plane = {}

        def load_x(z, j, n):
            if n == 1:
                rows = laid.tile([P, n, T], F32, name=f"x{z}{j}", offset=PLANE_BYTES * (j - 2), align_bytes=256)
            else:
                rows = keep.tile([P, n, T], F32, name=f"x{z}{j}", align_bytes=256)
            nc.sync.dma_start(out=rows[:], in_=x_rows[z, :, j:j + n, :])
            for i in range(n):
                plane[z, j + i] = rows[:, i, :]

        def by_pass(w):
            return w.rearrange("(z p j) c -> p z j c", z=PASSES, j=PACK)

        g_raw = [keep.tile([P, PACK, N], F32, name=f"g_raw{z}", tag=f"g_raw{z}", align_bytes=256) for z in range(PASSES)]
        nc.sync.dma_start(out=g_raw[0][:], in_=by_pass(w1)[:, 0])
        nc.sync.dma_start(offs_t[:], offs)
        load_x(0, 0, PACK)
        load_x(1, 0, 2)
        load_x(1, 2, 1)
        load_x(1, 3, 1)
        nc.sync.dma_start(out=g_raw[1][:], in_=by_pass(w1)[:, 1])
        h_raw = [keep.tile([P, PACK, N], F32, name=f"h_raw{z}", tag=f"h_raw{z}", align_bytes=256) for z in range(PASSES)]
        for z in range(PASSES):
            nc.sync.dma_start(out=h_raw[z][:], in_=by_pass(w3)[:, z])
        s_raw = keep.tile([P, PASSES, PACK, N], F32, name="s_raw", align_bytes=256)
        for z in range(PASSES):
            nc.sync.dma_start(out=s_raw[:, z], in_=by_pass(w2)[:, z])
        nc.sync.dma_start(cen_t[:], cen)
        nc.sync.dma_start(pos1_t[:], pos1)
        nc.sync.dma_start(pos2_t[:], pos2)

        w_raw = {("g", z): g_raw[z][:] for z in range(PASSES)}
        w_raw.update({("h", z): h_raw[z][:] for z in range(PASSES)})
        w_raw.update({("s", z): s_raw[:, z] for z in range(PASSES)})
        s_il = keep.tile([P, PASSES, N, PACK], BF16, name="s_il", align_bytes=64)
        w_il = {("s", z): s_il[:, z] for z in range(PASSES)}
        for m in "gh":
            for z in range(PASSES):
                w_il[m, z] = keep.tile([P, N, PACK], BF16, name=f"wil_{m}{z}", align_bytes=64)[:]
        w_codes = {}
        w_scales = {}

        def round_w(piece, copy, c0=0, c1=N):
            copy(
                out=w_il[piece][:, c0:c1, :].rearrange("p (c i) j -> p c j i", i=4),
                in_=w_raw[piece][:, :, c0:c1].rearrange("p j (c i) -> p c j i", i=4),
            )

        def quant_w(piece):
            if piece == ("g", 0):
                w_codes[piece] = keep.tile([P, N], U32, name="wc_g0", tag="picked12", align_bytes=64)
            else:
                w_codes[piece] = keep.tile([P, N], U32, name=f"wc_{piece[0]}{piece[1]}", align_bytes=64)
            w_scales[piece] = keep.tile([P, N], U8, name=f"ws_{piece[0]}{piece[1]}", align_bytes=64)
            nc.vector.quantize_mx(
                out=w_codes[piece][:].bitcast(FP8X4),
                scales=w_scales[piece][:],
                in_=w_il[piece].rearrange("p c j -> p (c j)"),
            )

        x_codes = {}
        x_scales = [keep.tile([P, S], U8, name=f"xs{z}", align_bytes=64) for z in range(PASSES)]
        x_il = [keep.tile([P, S, PACK], BF16, name=f"xil{z}", align_bytes=64) for z in range(PASSES)]

        def listed(z, j, c, n):
            return plane[z, j].indirect(offs_t[:, c // COLS16:(c + n) // COLS16])

        def gather_planes(z, j0, n, on_vector):
            picked = {c: keep.tile([P, n, HALF], F32, name=f"picked{z}{j0}_{c}") for c in (0, HALF)}
            for c, nv in zip(picked, on_vector):
                for i in range(nv):
                    nc.vector.tensor_copy(out=picked[c][:, i, :], in_=listed(z, j0 + i, c, HALF))
                for i in range(nv, n):
                    nc.scalar.activation(out=picked[c][:, i, :], in_=listed(z, j0 + i, c, HALF), func=ACT.Copy)
            for c in picked:
                nc.vector.tensor_copy(
                    out=x_il[z][:, c:c + HALF, j0:j0 + n].rearrange("p (c i) j -> p c j i", i=4),
                    in_=picked[c][:].rearrange("p j (c i) -> p c j i", i=4),
                )

        def gather_plane(z, j):
            picked = keep.tile([P, HALF], F32, name=f"picked{z}{j}", tag=f"picked{z}{j}", align_bytes=64)
            nc.vector.tensor_copy(out=x_il[z][:, :HALF, j], in_=listed(z, j, 0, HALF))
            nc.scalar.activation(out=picked[:], in_=listed(z, j, HALF, HALF), func=ACT.Copy)
            nc.vector.tensor_copy(out=x_il[z][:, HALF:, j], in_=picked[:])

        def quant_x(z, c, codes):
            x_codes[z, c] = codes
            nc.vector.quantize_mx(
                out=codes.bitcast(FP8X4),
                scales=x_scales[z][:, c:c + HALF],
                in_=x_il[z][:, c:c + HALF, :].rearrange("p c j -> p (c j)"),
            )

        halves = (0, HALF)
        banks = {}
        prod = {}

        def product(m, z):
            for c in halves:
                if z == 0:
                    banks[m, c] = psum.tile([P, HALF], F32, name=f"bank_{m}{c}")
                nc.tensor.matmul_mx(
                    out=banks[m, c][:],
                    lhsT=w_codes[m, z][:].bitcast(FP8X4),
                    lhsT_scale=w_scales[m, z][:],
                    rhs=x_codes[z, c].bitcast(FP8X4),
                    rhs_scale=x_scales[z][:, c:c + HALF],
                    start=(z == 0),
                    stop=(z == PASSES - 1),
                )

        def leave_psum(m, tag):
            prod[m] = keep.tile([P, S], F32, name=f"{m}_sb", tag=tag, align_bytes=64)
            for c in halves:
                nc.scalar.copy(out=prod[m][:, c:c + HALF], in_=banks[m, c][:])

        round_w(("g", 0), nc.scalar.copy)
        gather_planes(0, 0, PACK, (2, 2))
        first_codes = keep.tile([P, S], U32, name="xc0", align_bytes=64)
        for c in halves:
            quant_x(0, c, first_codes[:, c:c + HALF])
        gather_planes(1, 0, 2, (1, 1))
        gather_plane(1, 2)
        quant_w(("g", 0))
        product("g", 0)
        for c in halves:
            unread = psum.tile([32, S], F32, name=f"unread{c}")
            nc.tensor.matmul_mx(
                out=unread[:],
                lhsT=w_codes["g", 0][:, :32].bitcast(FP8X4),
                lhsT_scale=w_scales["g", 0][:, :32],
                rhs=first_codes[:].bitcast(FP8X4),
                rhs_scale=x_scales[0][:],
                start=True,
                stop=True,
            )
        gather_plane(1, 3)
        quant_x(1, 0, laid.tile([P, HALF], U32, name="xc1a", offset=PLANE_BYTES, align_bytes=64)[:])
        round_w(("g", 1), nc.scalar.copy)
        quant_w(("g", 1))
        quant_x(1, HALF, keep.tile([P, HALF], U32, name="xc1b", tag="g_raw1", align_bytes=256)[:])
        product("g", 1)
        round_w(("h", 0), nc.scalar.copy)
        round_w(("h", 1), nc.vector.tensor_copy, 0, 48)
        round_w(("h", 1), nc.scalar.copy, 48, N)
        for z in range(PASSES):
            quant_w(("h", z))
            product("h", z)
        leave_psum("g", "g_sb")
        most = N - 8
        round_w(("s", 0), nc.vector.tensor_copy, 0, most)
        nc.vector.tensor_copy(
            out=s_il[:, :, most:, :].rearrange("p z (c i) j -> p z c j i", i=4),
            in_=s_raw[:, :, :, most:].rearrange("p z j (c i) -> p z c j i", i=4),
        )
        round_w(("s", 1), nc.vector.tensor_copy, 0, most)
        for z in range(PASSES):
            quant_w(("s", z))
            product("s", z)
        leave_psum("h", "h_sb")
        ends = [slice(0, V // 2), slice(V // 2, V)]
        a, b = ends

        def fetched(m, places, v):
            return prod[m][:].indirect(places[:, v.start // COLS16:v.stop // COLS16])

        cut = V // 4
        few, many = slice(0, cut), slice(cut, V)
        gc_a = keep.tile([P, cut], F32, name="gc_a", tag="gc_a")
        gc_b = keep.tile([P, V - cut], F32, name="gc_b")
        nc.vector.tensor_copy(out=gc_a[:], in_=fetched("g", cen_t, few))
        nc.scalar.activation(out=gc_b[:], in_=fetched("g", cen_t, many), func=ACT.Copy)
        leave_psum("s", "s_sb")

        t1 = keep.tile([P, V], F32, name="t1")
        t2 = keep.tile([P, V], F32, name="t2")
        for v, gc in ((few, gc_a), (many, gc_b)):
            for t, places in ((t1, pos1_t), (t2, pos2_t)):
                nc.vector.tensor_tensor(t[:, v], fetched("h", places, v), gc[:], ALU.mult)

        u1_a = keep.tile([P, V // 2], F32, name="u1_a", tag="gc_a")
        u1_b = keep.tile([P, V // 2], F32, name="u1_b")
        r1 = keep.tile([P, V], F32, name="r1")
        u2 = keep.tile([P, V], F32, name="u2")
        sc = keep.tile([P, V], F32, name="sc")
        res = keep.tile([P, V], F32, name="res", align_bytes=256)
        for v in (b, a):
            nc.scalar.activation(out=sc[:, v], in_=fetched("s", cen_t, v), func=ACT.Copy)
        nc.vector.tensor_tensor(u1_a[:], fetched("s", cen_t, a), t1[:, a], ALU.add)
        nc.vector.tensor_tensor(u1_b[:], sc[:, b], t1[:, b], ALU.add)
        for v in (a, b):
            nc.vector.tensor_tensor(u2[:, v], sc[:, v], t2[:, v], ALU.add)
        for v, u1 in ((a, u1_a), (b, u1_b)):
            nc.scalar.activation(out=r1[:, v], in_=u1[:], func=ACT.Relu)
            nc.vector.scalar_tensor_tensor(out=res[:, v], in0=u2[:, v], scalar=0.0, in1=r1[:, v], op0=ALU.max, op1=ALU.add)
            nc.sync.dma_start(out=out[:, v], in_=res[:, v])
